import numpy as np
import ml_dtypes


def mxq(x, axis, fmt="e4m3"):
    dtype, down = {"e4m3": (ml_dtypes.float8_e4m3fn, 7), "e5m2": (ml_dtypes.float8_e5m2, 14)}[fmt]
    v = np.moveaxis(np.asarray(x, np.float32).astype(ml_dtypes.bfloat16).astype(np.float64), axis, -1)
    blocks = v.reshape(v.shape[:-1] + (-1, 32))
    amax = np.abs(blocks).max(-1, keepdims=True)
    byte = np.maximum(np.where(amax > 0, np.frexp(amax)[1] - 1 + 127, 0) - down, 1)
    scale = np.exp2(byte - 127.0)
    codes = (blocks / scale).astype(np.float32).astype(dtype).astype(np.float64)
    return np.moveaxis((codes * scale).reshape(v.shape), -1, axis)


WIDE = False


def mx_kscale(k):
    if not WIDE:
        return np.ones(k)
    levels = np.array([10, -10, 5, -5, 0])
    if k % 512:
        return np.exp2(np.random.permutation(np.resize(levels, k // 32))).repeat(32)
    a = np.empty((k // 512, 16))
    for p in range(k // 512):
        a[p, :8] = np.random.permutation(np.resize(levels, 8))
        for g in range(8):
            far = levels[np.abs(levels - a[p, g]) >= 10]
            a[p, g + 8] = far[np.random.randint(len(far))]
    return np.exp2(a.ravel()).repeat(32)


def f64(x):
    return np.asarray(x).astype(np.float64)


def striped(idx):
    return np.tile(idx.reshape(-1, 16).T, (8, 1)).astype(np.uint16)


def unstriped(offs):
    return offs[:16].T.reshape(-1).astype(np.int64)


E2M1 = np.array([0.0, 0.5, 1.0, 1.5, 2.0, 3.0, 4.0, 6.0, -0.0, -0.5, -1.0, -1.5, -2.0, -3.0, -4.0, -6.0])


def pack_fp4(w):
    k, n = w.shape
    w = f64(np.asarray(w, np.float32).astype(ml_dtypes.bfloat16)).reshape(k // 32, 32, n)
    amax = np.abs(w).max(1)
    mant, ex = np.frexp(amax / 6.0)
    byte = np.clip(np.where(amax > 0, np.where(mant > 0.5, ex, ex - 1) + 127, 1), 1, 254)
    scaled = (w * np.exp2(127.0 - byte)[:, None, :]).reshape(k, n).astype(np.float32)
    c = np.ascontiguousarray(scaled.reshape(k // 512, 128, 4, n).transpose(0, 1, 3, 2)).astype(ml_dtypes.float4_e2m1fn).view(np.uint8) & 0xF
    words = (c[..., 0::2] | (c[..., 1::2] << 4)).reshape(k // 512, 128, 2 * n)
    return np.ascontiguousarray(words), np.ascontiguousarray(byte.astype(np.uint8).reshape(k // 512, 16, n))


def unpack_fp4(words, scales):
    g, _, n = scales.shape
    words = np.ascontiguousarray(words).reshape(g, 128, n, 2)
    nib = np.empty((g, 128, n, 4), np.uint8)
    nib[..., 0::2] = words & 0xF
    nib[..., 1::2] = words >> 4
    vals = E2M1[nib] * np.repeat(np.exp2(scales.astype(np.float64) - 127.0), 8, axis=1)[..., None]
    return vals.transpose(0, 1, 3, 2).reshape(g * 512, n)


def silu(v):
    return v / (1.0 + np.exp(-np.maximum(v, -700.0)))


K, T, S, H, N, U = 512, 2048, 1024, 512, 128, 2048
P = 2 ** 7


def setup_inputs():
    n = np.random.standard_normal
    s = mx_kscale(K)[:, None]
    u = mx_kscale(H)
    packed_xT = pack_fp4(n((K, T)) * s)
    return {
        "x_words": packed_xT[0],
        "x_scales": packed_xT[1],
        "gate": np.tile(np.random.uniform(0.5, 1.5, S), (P, 1)).astype(np.float32),
        "w1": (n((K, H)) / np.sqrt(K) / s).astype(np.float32),
        "w3": (n((K, H)) / np.sqrt(K) / s * u).astype(np.float32),
        "w2": (n((H, N)) / np.sqrt(H) / u[:, None]).astype(np.float32),
        "offs": striped(np.random.permutation(T)[:S]),
        "dst": striped(np.random.permutation(U)[:S]),
    }


def reference(x_words, x_scales, gate, w1, w3, w2, offs, dst):
    xq = unpack_fp4(x_words, x_scales)[:, unstriped(offs)]
    h = (silu(mxq(f64(w1), 0, "e4m3").T @ xq)) * ((mxq(f64(w3), 0, "e4m3").T @ xq))
    y = mxq(f64(w2), 0, "e4m3").T @ mxq(h, 0, "e4m3")
    out = np.zeros((N, U))
    out[:, unstriped(dst)] = y * f64(gate)[:1]
    return out

@@ -1,0 +1,178 @@
+from contextlib import ExitStack
+
+import concourse.mybir as mybir
+
+K, T, S, H, N, U = 512, 2048, 1024, 512, 128, 2048
+FLOPS = 2 * S * (2 * K * H + H * N)
+
+F32 = mybir.dt.float32
+BF16 = mybir.dt.bfloat16
+I32 = mybir.dt.int32
+U32 = mybir.dt.uint32
+U16 = mybir.dt.uint16
+U8 = mybir.dt.uint8
+FP8X4 = mybir.dt.float8_e4m3fn_x4
+FP4X4 = mybir.dt.float4_e2m1fn_x4
+SILU = mybir.ActivationFunctionType.Silu
+MULT = mybir.AluOpType.mult
+
+P = 128
+PACK = 4
+PER_COL = 16
+GATHER = 512
+CHUNK = 128
+GROUP = 256
+HALF = H // 2
+
+
+def tile_picked_route2_glusilu_p_kernel(
+    tc, x_words, x_scales, gate, w1, w3, w2, offs, dst, out
+):
+    nc = tc.nc
+    with ExitStack() as ctx:
+        keep = ctx.enter_context(tc.tile_pool(name="keep", bufs=1))
+        stage = ctx.enter_context(tc.tile_pool(name="stage", bufs=1))
+        ring = ctx.enter_context(tc.tile_pool(name="ring", bufs=3))
+        psum = ctx.enter_context(tc.psum_pool(name="psum", bufs=3))
+        psum_y = ctx.enter_context(tc.psum_pool(name="psum_y", bufs=2))
+
+        offs_sb = keep.tile([P, S // PER_COL], U16, name="offs_sb")
+        dst_sb = keep.tile([P, S // PER_COL], U16, name="dst_sb")
+        word_table = keep.tile([P, T], U16, name="word_table", align_bytes=64)
+        scale_table = keep.tile([P, T], U8, name="scale_table", align_bytes=64)
+        window = keep.tile([P, U], F32, name="window", align_bytes=64)
+        warm = stage.tile([P, 8], F32, name="warm", tag="slot2", align_bytes=64)
+
+        nc.gpsimd.memset(warm[:], 0.0)
+        nc.gpsimd.memset(scale_table[:].bitcast(I32), 0)
+        nc.scalar.activation(warm[:, 0:1], warm[:, 1:2], SILU)
+        nc.gpsimd.memset(window[:], 0.0)
+
+        nc.sync.dma_start(out=word_table[:].bitcast(I32), in_=x_words[0].bitcast(I32))
+        nc.sync.dma_start(offs_sb[:], offs)
+        nc.sync.dma_start(dst_sb[:], dst)
+        for q in range(4):
+            nc.sync.dma_start(
+                out=scale_table[32 * q : 32 * q + 4, :].bitcast(I32),
+                in_=x_scales[0, 4 * q : 4 * q + 4, :].bitcast(I32),
+            )
+        def load_half(tile, w, u):
+            nc.sync.dma_start(
+                out=tile, in_=w[:, u * HALF : (u + 1) * HALF].rearrange("(p j) c -> p j c", j=PACK)
+            )
+
+        raw = {}
+        for u in range(2):
+            raw["w1", u] = stage.tile([P, PACK, HALF], F32, name=f"w1_raw{u}", tag=f"slot{u}", align_bytes=64)[:]
+            load_half(raw["w1", u], w1, u)
+        w3_raw = stage.tile([P, 2, PACK, HALF], F32, name="w3_raw", tag="slot2", align_bytes=64)
+        for u in range(2):
+            raw["w3", u] = w3_raw[:, u]
+            load_half(raw["w3", u], w3, u)
+
+        def pick(g, table, tile):
+            cols = slice(g * GATHER // PER_COL, (g + 1) * GATHER // PER_COL)
+            nc.vector.tensor_copy(tile[:], table[:].indirect(offs_sb[:, cols]))
+            return tile
+
+        x_codes = [
+            pick(g, word_table, keep.tile([P, GATHER], U16, name=f"x_codes{g}", align_bytes=64))
+            for g in range(S // GATHER)
+        ]
+        x_bytes = [pick(0, scale_table, keep.tile([P, GATHER], U8, name="x_bytes0", align_bytes=64))]
+
+        codes, scales = {}, {}
+        for name in ("w1", "w3"):
+            grouped = stage.tile([P, PACK, P, PACK], BF16, name=f"{name}_grouped", tag=f"{name}_grouped", align_bytes=64)
+            for u in range(2):
+                src = raw[name, u].rearrange("p j (m t) -> p m t j", t=PACK)
+                dstv = grouped[:, :, 64 * u : 64 * (u + 1), :].rearrange("p t m j -> p m t j")
+                if name == "w3" and u == 1:
+                    nc.vector.tensor_copy(dstv, src)
+                else:
+                    nc.scalar.copy(dstv, src)
+                if name == "w1" and u == 0:
+                    w2_raw = stage.tile([P, PACK, N], F32, name="w2_raw", tag="slot0", align_bytes=64)
+                    nc.sync.dma_start(out=w2_raw[:], in_=w2.rearrange("(p j) c -> p j c", j=PACK))
+                if name == "w1" and u == 1:
+                    gate_sb = stage.tile([P, S], F32, name="gate_sb", tag="slot1", align_bytes=64)
+                    nc.sync.dma_start(out=gate_sb[:], in_=gate)
+            codes[name] = keep.tile([P, H], U32, name=f"{name}_codes", align_bytes=64)
+            scales[name] = keep.tile([P, H], U8, name=f"{name}_scales", align_bytes=64)
+            nc.vector.quantize_mx(
+                out=codes[name][:].bitcast(FP8X4),
+                scales=scales[name][:],
+                in_=grouped[:].rearrange("p t m j -> p (t m j)"),
+            )
+
+        x_bytes.append(
+            pick(1, scale_table, stage.tile([P, GATHER], U8, name="x_bytes1", tag="w3_grouped", align_bytes=64))
+        )
+
+        w2_grouped = keep.tile([P, N, PACK], BF16, name="w2_grouped", align_bytes=64)
+        w2_codes = keep.tile([P, N], U32, name="w2_codes", align_bytes=64)
+        w2_scales = keep.tile([P, N], U8, name="w2_scales", align_bytes=64)
+
+        def product(name, c):
+            bank = psum.tile([P, PACK, CHUNK], F32, name=f"{name}_bank")
+            g, first = divmod(c * CHUNK, GATHER)
+            for t in range(PACK):
+                nc.tensor.matmul_mx(
+                    out=bank[:, t, :],
+                    lhsT=codes[name][:, t * P : (t + 1) * P].bitcast(FP8X4),
+                    lhsT_scale=scales[name][:, t * P : (t + 1) * P],
+                    rhs=x_codes[g][:, first : first + CHUNK].bitcast(FP4X4),
+                    rhs_scale=x_bytes[g][:, first : first + CHUNK],
+                    start=True,
+                    stop=True,
+                )
+            return bank[:].rearrange("p t n -> p n t")
+
+        y_sb = []
+        for g in range(S // GROUP):
+            h = keep.tile([P, GROUP, PACK], BF16, name=f"h{g}", align_bytes=64)
+            for i in range(GROUP // CHUNK):
+                c = g * (GROUP // CHUNK) + i
+                a = product("w1", c)
+                act = ring.tile([P, CHUNK, PACK], F32, name="act", align_bytes=64)
+                nc.scalar.activation(act[:], a, SILU)
+                b = product("w3", c)
+                nc.vector.tensor_tensor(h[:, i * CHUNK : (i + 1) * CHUNK, :], b, act[:], MULT)
+            if g == 0:
+                nc.scalar.copy(
+                    w2_grouped[:].rearrange("p (c i) j -> p c j i", i=4),
+                    w2_raw[:].rearrange("p j (c i) -> p c j i", i=4),
+                )
+                nc.vector.quantize_mx(
+                    out=w2_codes[:].bitcast(FP8X4),
+                    scales=w2_scales[:],
+                    in_=w2_grouped[:].rearrange("p n j -> p (n j)"),
+                )
+            h_codes = keep.tile([P, GROUP], U32, name=f"h_codes{g}", align_bytes=64)
+            h_scales = keep.tile([P, GROUP], U8, name=f"h_scales{g}", align_bytes=64)
+            nc.vector.quantize_mx(
+                out=h_codes[:].bitcast(FP8X4),
+                scales=h_scales[:],
+                in_=h[:].rearrange("p n t -> p (n t)"),
+            )
+            y = psum_y.tile([P, GROUP], F32, name="y")
+            nc.tensor.matmul_mx(
+                out=y[:],
+                lhsT=w2_codes[:].bitcast(FP8X4),
+                lhsT_scale=w2_scales[:],
+                rhs=h_codes[:].bitcast(FP8X4),
+                rhs_scale=h_scales[:],
+                start=True,
+                stop=True,
+            )
+            y_sb.append(keep.tile([P, GROUP], F32, name=f"y_sb{g}", align_bytes=64))
+            nc.scalar.copy(y_sb[g][:], y[:])
+
+        for g in range(S // GROUP):
+            cols = slice(g * GROUP // PER_COL, (g + 1) * GROUP // PER_COL)
+            nc.vector.tensor_tensor(
+                window[:].indirect(dst_sb[:, cols]), y_sb[g][:], gate_sb[:, g * GROUP : (g + 1) * GROUP], MULT
+            )
+
+        nc.sync.dma_start(out=out[:, 0 : U // 2], in_=window[:, 0 : U // 2])
+        nc.scalar.dma_start(out=out[:, U // 2 : U], in_=window[:, U // 2 : U])

@@ -22,6 +22,7 @@ PER_COL = 16
 GATHER = 512
 CHUNK = 128
 GROUP = 256
+SCATTER = 512
 HALF = H // 2
 
 
@@ -32,9 +33,8 @@ def tile_picked_route2_glusilu_p_kernel(
     with ExitStack() as ctx:
         keep = ctx.enter_context(tc.tile_pool(name="keep", bufs=1))
         stage = ctx.enter_context(tc.tile_pool(name="stage", bufs=1))
-        ring = ctx.enter_context(tc.tile_pool(name="ring", bufs=3))
         psum = ctx.enter_context(tc.psum_pool(name="psum", bufs=3))
-        psum_y = ctx.enter_context(tc.psum_pool(name="psum_y", bufs=2))
+        psum_y = ctx.enter_context(tc.psum_pool(name="psum_y", bufs=1))
 
         offs_sb = keep.tile([P, S // PER_COL], U16, name="offs_sb")
         dst_sb = keep.tile([P, S // PER_COL], U16, name="dst_sb")
@@ -43,13 +43,13 @@ def tile_picked_route2_glusilu_p_kernel(
         window = keep.tile([P, U], F32, name="window", align_bytes=64)
         warm = stage.tile([P, 8], F32, name="warm", tag="slot2", align_bytes=64)
 
-        nc.gpsimd.memset(warm[:], 0.0)
-        nc.gpsimd.memset(scale_table[:].bitcast(I32), 0)
+        nc.vector.memset(warm[:], 0.0)
+        nc.vector.memset(scale_table[:].bitcast(I32), 0)
         nc.scalar.activation(warm[:, 0:1], warm[:, 1:2], SILU)
-        nc.gpsimd.memset(window[:], 0.0)
+        nc.vector.memset(window[:], 0.0)
 
-        nc.sync.dma_start(out=word_table[:].bitcast(I32), in_=x_words[0].bitcast(I32))
         nc.sync.dma_start(offs_sb[:], offs)
+        nc.sync.dma_start(out=word_table[:].bitcast(I32), in_=x_words[0].bitcast(I32))
         nc.sync.dma_start(dst_sb[:], dst)
         for q in range(4):
             nc.sync.dma_start(
@@ -61,14 +61,12 @@ def tile_picked_route2_glusilu_p_kernel(
                 out=tile, in_=w[:, u * HALF : (u + 1) * HALF].rearrange("(p j) c -> p j c", j=PACK)
             )
 
-        raw = {}
-        for u in range(2):
-            raw["w1", u] = stage.tile([P, PACK, HALF], F32, name=f"w1_raw{u}", tag=f"slot{u}", align_bytes=64)[:]
-            load_half(raw["w1", u], w1, u)
-        w3_raw = stage.tile([P, 2, PACK, HALF], F32, name="w3_raw", tag="slot2", align_bytes=64)
-        for u in range(2):
-            raw["w3", u] = w3_raw[:, u]
-            load_half(raw["w3", u], w3, u)
+        first_raw = stage.tile([P, PACK, HALF], F32, name="first_raw", tag="slot0", align_bytes=64)
+        later_raw = stage.tile([P, 3, PACK, HALF], F32, name="later_raw", tag="slot2", align_bytes=64)
+        raw = {("w1", 0): first_raw[:], ("w1", 1): later_raw[:, 0], ("w3", 0): later_raw[:, 1], ("w3", 1): later_raw[:, 2]}
+        for name, w in (("w1", w1), ("w3", w3)):
+            for u in range(2):
+                load_half(raw[name, u], w, u)
 
         def pick(g, table, tile):
             cols = slice(g * GATHER // PER_COL, (g + 1) * GATHER // PER_COL)
@@ -85,8 +83,8 @@ def tile_picked_route2_glusilu_p_kernel(
         for name in ("w1", "w3"):
             grouped = stage.tile([P, PACK, P, PACK], BF16, name=f"{name}_grouped", tag=f"{name}_grouped", align_bytes=64)
             for u in range(2):
-                src = raw[name, u].rearrange("p j (m t) -> p m t j", t=PACK)
-                dstv = grouped[:, :, 64 * u : 64 * (u + 1), :].rearrange("p t m j -> p m t j")
+                src = raw[name, u].rearrange("p j (m t) -> p m j t", t=PACK)
+                dstv = grouped[:, :, 64 * u : 64 * (u + 1), :].rearrange("p t m j -> p m j t")
                 if name == "w3" and u == 1:
                     nc.vector.tensor_copy(dstv, src)
                 else:
@@ -94,9 +92,6 @@ def tile_picked_route2_glusilu_p_kernel(
                 if name == "w1" and u == 0:
                     w2_raw = stage.tile([P, PACK, N], F32, name="w2_raw", tag="slot0", align_bytes=64)
                     nc.sync.dma_start(out=w2_raw[:], in_=w2.rearrange("(p j) c -> p j c", j=PACK))
-                if name == "w1" and u == 1:
-                    gate_sb = stage.tile([P, S], F32, name="gate_sb", tag="slot1", align_bytes=64)
-                    nc.sync.dma_start(out=gate_sb[:], in_=gate)
             codes[name] = keep.tile([P, H], U32, name=f"{name}_codes", align_bytes=64)
             scales[name] = keep.tile([P, H], U8, name=f"{name}_scales", align_bytes=64)
             nc.vector.quantize_mx(
@@ -105,6 +100,8 @@ def tile_picked_route2_glusilu_p_kernel(
                 in_=grouped[:].rearrange("p t m j -> p (t m j)"),
             )
 
+        gate_sb = stage.tile([P, S], F32, name="gate_sb", tag="w1_grouped", align_bytes=64)
+        nc.sync.dma_start(out=gate_sb[:], in_=gate)
         x_bytes.append(
             pick(1, scale_table, stage.tile([P, GATHER], U8, name="x_bytes1", tag="w3_grouped", align_bytes=64))
         )
@@ -128,36 +125,28 @@ def tile_picked_route2_glusilu_p_kernel(
                 )
             return bank[:].rearrange("p t n -> p n t")
 
-        y_sb = []
-        for g in range(S // GROUP):
-            h = keep.tile([P, GROUP, PACK], BF16, name=f"h{g}", align_bytes=64)
-            for i in range(GROUP // CHUNK):
-                c = g * (GROUP // CHUNK) + i
-                a = product("w1", c)
-                act = ring.tile([P, CHUNK, PACK], F32, name="act", align_bytes=64)
-                nc.scalar.activation(act[:], a, SILU)
-                b = product("w3", c)
-                nc.vector.tensor_tensor(h[:, i * CHUNK : (i + 1) * CHUNK, :], b, act[:], MULT)
-            if g == 0:
-                nc.scalar.copy(
-                    w2_grouped[:].rearrange("p (c i) j -> p c j i", i=4),
-                    w2_raw[:].rearrange("p j (c i) -> p c j i", i=4),
-                )
-                nc.vector.quantize_mx(
-                    out=w2_codes[:].bitcast(FP8X4),
-                    scales=w2_scales[:],
-                    in_=w2_grouped[:].rearrange("p n j -> p (n j)"),
-                )
+        h = [keep.tile([P, GROUP, PACK], BF16, name=f"h{g}", align_bytes=64) for g in range(S // GROUP)]
+        y = [psum_y.tile([P, SCATTER], F32, name=f"y{s}") for s in range(S // SCATTER)]
+
+        def hidden(c):
+            g, i = divmod(c, GROUP // CHUNK)
+            a = product("w1", c)
+            act = stage.tile([P, CHUNK, PACK], F32, name=f"act{c}", tag=f"act{c}", align_bytes=64)
+            nc.scalar.activation(act[:], a, SILU)
+            b = product("w3", c)
+            nc.vector.tensor_tensor(h[g][:, i * CHUNK : (i + 1) * CHUNK, :], b, act[:], MULT)
+
+        def second(g):
             h_codes = keep.tile([P, GROUP], U32, name=f"h_codes{g}", align_bytes=64)
             h_scales = keep.tile([P, GROUP], U8, name=f"h_scales{g}", align_bytes=64)
             nc.vector.quantize_mx(
                 out=h_codes[:].bitcast(FP8X4),
                 scales=h_scales[:],
-                in_=h[:].rearrange("p n t -> p (n t)"),
+                in_=h[g][:].rearrange("p n t -> p (n t)"),
             )
-            y = psum_y.tile([P, GROUP], F32, name="y")
+            s, first = divmod(g * GROUP, SCATTER)
             nc.tensor.matmul_mx(
-                out=y[:],
+                out=y[s][:, first : first + GROUP],
                 lhsT=w2_codes[:].bitcast(FP8X4),
                 lhsT_scale=w2_scales[:],
                 rhs=h_codes[:].bitcast(FP8X4),
@@ -165,13 +154,30 @@ def tile_picked_route2_glusilu_p_kernel(
                 start=True,
                 stop=True,
             )
-            y_sb.append(keep.tile([P, GROUP], F32, name=f"y_sb{g}", align_bytes=64))
-            nc.scalar.copy(y_sb[g][:], y[:])
 
-        for g in range(S // GROUP):
-            cols = slice(g * GROUP // PER_COL, (g + 1) * GROUP // PER_COL)
+        hidden(0)
+        nc.scalar.copy(
+            w2_grouped[:].rearrange("p (c i) j -> p c j i", i=4),
+            w2_raw[:].rearrange("p j (c i) -> p c j i", i=4),
+        )
+        nc.vector.quantize_mx(
+            out=w2_codes[:].bitcast(FP8X4),
+            scales=w2_scales[:],
+            in_=w2_grouped[:].rearrange("p n j -> p (n j)"),
+        )
+        for c in range(1, 8):
+            hidden(c)
+            if c in (2, 4):
+                second(c // 2 - 1)
+        second(2)
+        second(3)
+
+        for s in range(S // SCATTER):
+            y_sb = stage.tile([P, SCATTER], F32, name=f"y_sb{s}", tag=f"act{6 + s}", align_bytes=64)
+            nc.scalar.copy(y_sb[:], y[s][:])
+            cols = slice(s * SCATTER // PER_COL, (s + 1) * SCATTER // PER_COL)
             nc.vector.tensor_tensor(
-                window[:].indirect(dst_sb[:, cols]), y_sb[g][:], gate_sb[:, g * GROUP : (g + 1) * GROUP], MULT
+                window[:].indirect(dst_sb[:, cols]), y_sb[:], gate_sb[:, s * SCATTER : (s + 1) * SCATTER], MULT
             )
 
         nc.sync.dma_start(out=out[:, 0 : U // 2], in_=window[:, 0 : U // 2])

@@ -33,8 +33,7 @@ def tile_picked_route2_glusilu_p_kernel(
     with ExitStack() as ctx:
         keep = ctx.enter_context(tc.tile_pool(name="keep", bufs=1))
         stage = ctx.enter_context(tc.tile_pool(name="stage", bufs=1))
-        psum = ctx.enter_context(tc.psum_pool(name="psum", bufs=3))
-        psum_y = ctx.enter_context(tc.psum_pool(name="psum_y", bufs=1))
+        psum = ctx.enter_context(tc.psum_pool(name="psum", bufs=1))
 
         offs_sb = keep.tile([P, S // PER_COL], U16, name="offs_sb")
         dst_sb = keep.tile([P, S // PER_COL], U16, name="dst_sb")
@@ -68,16 +67,28 @@ def tile_picked_route2_glusilu_p_kernel(
             for u in range(2):
                 load_half(raw[name, u], w, u)
 
-        def pick(g, table, tile):
-            cols = slice(g * GATHER // PER_COL, (g + 1) * GATHER // PER_COL)
+        def pick(table, tile, first, count):
+            cols = slice(first // PER_COL, (first + count) // PER_COL)
             nc.vector.tensor_copy(tile[:], table[:].indirect(offs_sb[:, cols]))
-            return tile
 
-        x_codes = [
-            pick(g, word_table, keep.tile([P, GATHER], U16, name=f"x_codes{g}", align_bytes=64))
-            for g in range(S // GATHER)
-        ]
-        x_bytes = [pick(0, scale_table, keep.tile([P, GATHER], U8, name="x_bytes0", align_bytes=64))]
+        x_codes, x_bytes = {}, {}
+
+        def pick_words(chunks):
+            tile = keep.tile([P, len(chunks) * CHUNK], U16, name=f"x_codes{chunks[0]}", align_bytes=64)
+            pick(word_table, tile, chunks[0] * CHUNK, len(chunks) * CHUNK)
+            for i, c in enumerate(chunks):
+                x_codes[c] = tile[:, i * CHUNK : (i + 1) * CHUNK]
+
+        def pick_bytes(chunks, tag):
+            tile = stage.tile([P, len(chunks) * CHUNK], U8, name=f"x_bytes{chunks[0]}", tag=tag, align_bytes=64)
+            pick(scale_table, tile, chunks[0] * CHUNK, len(chunks) * CHUNK)
+            for i, c in enumerate(chunks):
+                x_bytes[c] = tile[:, i * CHUNK : (i + 1) * CHUNK]
+
+        pick_words(range(0, 4))
+        pick_words(range(4, 8))
+        pick_bytes(range(0, 3), "bytes_first")
+        pick_bytes(range(6, 8), "bytes_last")
 
         codes, scales = {}, {}
         for name in ("w1", "w3"):
@@ -102,31 +113,28 @@ def tile_picked_route2_glusilu_p_kernel(
 
         gate_sb = stage.tile([P, S], F32, name="gate_sb", tag="w1_grouped", align_bytes=64)
         nc.sync.dma_start(out=gate_sb[:], in_=gate)
-        x_bytes.append(
-            pick(1, scale_table, stage.tile([P, GATHER], U8, name="x_bytes1", tag="w3_grouped", align_bytes=64))
-        )
+        pick_bytes(range(3, 6), "slot2")
 
-        w2_grouped = keep.tile([P, N, PACK], BF16, name="w2_grouped", align_bytes=64)
         w2_codes = keep.tile([P, N], U32, name="w2_codes", align_bytes=64)
         w2_scales = keep.tile([P, N], U8, name="w2_scales", align_bytes=64)
 
         def product(name, c):
-            bank = psum.tile([P, PACK, CHUNK], F32, name=f"{name}_bank")
-            g, first = divmod(c * CHUNK, GATHER)
+            tag = f"a{c % 3}" if name == "w1" else f"b{c % 5}"
+            bank = psum.tile([P, PACK, CHUNK], F32, name=f"{name}_bank{c}", tag=tag)
             for t in range(PACK):
                 nc.tensor.matmul_mx(
                     out=bank[:, t, :],
                     lhsT=codes[name][:, t * P : (t + 1) * P].bitcast(FP8X4),
                     lhsT_scale=scales[name][:, t * P : (t + 1) * P],
-                    rhs=x_codes[g][:, first : first + CHUNK].bitcast(FP4X4),
-                    rhs_scale=x_bytes[g][:, first : first + CHUNK],
+                    rhs=x_codes[c].bitcast(FP4X4),
+                    rhs_scale=x_bytes[c],
                     start=True,
                     stop=True,
                 )
             return bank[:].rearrange("p t n -> p n t")
 
         h = [keep.tile([P, GROUP, PACK], BF16, name=f"h{g}", align_bytes=64) for g in range(S // GROUP)]
-        y = [psum_y.tile([P, SCATTER], F32, name=f"y{s}") for s in range(S // SCATTER)]
+        h_mx = []
 
         def hidden(c):
             g, i = divmod(c, GROUP // CHUNK)
@@ -144,37 +152,42 @@ def tile_picked_route2_glusilu_p_kernel(
                 scales=h_scales[:],
                 in_=h[g][:].rearrange("p n t -> p (n t)"),
             )
-            s, first = divmod(g * GROUP, SCATTER)
-            nc.tensor.matmul_mx(
-                out=y[s][:, first : first + GROUP],
-                lhsT=w2_codes[:].bitcast(FP8X4),
-                lhsT_scale=w2_scales[:],
-                rhs=h_codes[:].bitcast(FP8X4),
-                rhs_scale=h_scales[:],
-                start=True,
-                stop=True,
-            )
+            h_mx.append((h_codes, h_scales))
 
-        hidden(0)
-        nc.scalar.copy(
-            w2_grouped[:].rearrange("p (c i) j -> p c j i", i=4),
-            w2_raw[:].rearrange("p j (c i) -> p c j i", i=4),
-        )
-        nc.vector.quantize_mx(
-            out=w2_codes[:].bitcast(FP8X4),
-            scales=w2_scales[:],
-            in_=w2_grouped[:].rearrange("p n j -> p (n j)"),
-        )
-        for c in range(1, 8):
+        for c in range(8):
             hidden(c)
+            if c == 1:
+                w2_grouped = stage.tile([P, N, PACK], BF16, name="w2_grouped", tag="act0", align_bytes=64)
+                nc.scalar.copy(
+                    w2_grouped[:].rearrange("p (c i) j -> p c j i", i=4),
+                    w2_raw[:].rearrange("p j (c i) -> p c j i", i=4),
+                )
+            if c == 3:
+                nc.vector.quantize_mx(
+                    out=w2_codes[:].bitcast(FP8X4),
+                    scales=w2_scales[:],
+                    in_=w2_grouped[:].rearrange("p n j -> p (n j)"),
+                )
             if c in (2, 4):
                 second(c // 2 - 1)
         second(2)
         second(3)
 
         for s in range(S // SCATTER):
+            y = psum.tile([P, SCATTER], F32, name=f"y{s}", tag=f"b{s}")
+            for i in range(SCATTER // GROUP):
+                h_codes, h_scales = h_mx[s * (SCATTER // GROUP) + i]
+                nc.tensor.matmul_mx(
+                    out=y[:, i * GROUP : (i + 1) * GROUP],
+                    lhsT=w2_codes[:].bitcast(FP8X4),
+                    lhsT_scale=w2_scales[:],
+                    rhs=h_codes[:].bitcast(FP8X4),
+                    rhs_scale=h_scales[:],
+                    start=True,
+                    stop=True,
+                )
             y_sb = stage.tile([P, SCATTER], F32, name=f"y_sb{s}", tag=f"act{6 + s}", align_bytes=64)
-            nc.scalar.copy(y_sb[:], y[s][:])
+            nc.scalar.copy(y_sb[:], y[:])
             cols = slice(s * SCATTER // PER_COL, (s + 1) * SCATTER // PER_COL)
             nc.vector.tensor_tensor(
                 window[:].indirect(dst_sb[:, cols]), y_sb[:], gate_sb[:, s * SCATTER : (s + 1) * SCATTER], MULT

@@ -96,20 +96,22 @@ def tile_picked_route2_glusilu_p_kernel(
             for u in range(2):
                 src = raw[name, u].rearrange("p j (m t) -> p m j t", t=PACK)
                 dstv = grouped[:, :, 64 * u : 64 * (u + 1), :].rearrange("p t m j -> p m j t")
-                if name == "w3" and u == 1:
-                    nc.vector.tensor_copy(dstv, src)
-                else:
-                    nc.scalar.copy(dstv, src)
+                for t in (0, 2):
+                    if name == "w3" and u == 1:
+                        nc.vector.tensor_copy(dstv[:, :, :, t : t + 2], src[:, :, :, t : t + 2])
+                    else:
+                        nc.scalar.copy(dstv[:, :, :, t : t + 2], src[:, :, :, t : t + 2])
                 if name == "w1" and u == 0:
                     w2_raw = stage.tile([P, PACK, N], F32, name="w2_raw", tag="slot0", align_bytes=64)
                     nc.sync.dma_start(out=w2_raw[:], in_=w2.rearrange("(p j) c -> p j c", j=PACK))
             codes[name] = keep.tile([P, H], U32, name=f"{name}_codes", align_bytes=64)
             scales[name] = keep.tile([P, H], U8, name=f"{name}_scales", align_bytes=64)
-            nc.vector.quantize_mx(
-                out=codes[name][:].bitcast(FP8X4),
-                scales=scales[name][:],
-                in_=grouped[:].rearrange("p t m j -> p (t m j)"),
-            )
+            for t in (0, 2):
+                nc.vector.quantize_mx(
+                    out=codes[name][:, t * P : (t + 2) * P].bitcast(FP8X4),
+                    scales=scales[name][:, t * P : (t + 2) * P],
+                    in_=grouped[:, t : t + 2].rearrange("p t m j -> p (t m j)"),
+                )
 
         gate_sb = stage.tile([P, S], F32, name="gate_sb", tag="w1_grouped", align_bytes=64)
         nc.sync.dma_start(out=gate_sb[:], in_=gate)

@@ -44,13 +44,13 @@ def tile_picked_route2_glusilu_p_kernel(
 
         nc.vector.memset(warm[:], 0.0)
         nc.vector.memset(scale_table[:].bitcast(I32), 0)
-        nc.scalar.activation(warm[:, 0:1], warm[:, 1:2], SILU)
-        nc.vector.memset(window[:], 0.0)
+        nc.scalar.activation(window[:, 0:8], warm[:], SILU)
+        nc.vector.memset(window[:, 8:U], 0.0)
 
         nc.sync.dma_start(offs_sb[:], offs)
         nc.sync.dma_start(out=word_table[:].bitcast(I32), in_=x_words[0].bitcast(I32))
         nc.sync.dma_start(dst_sb[:], dst)
-        for q in range(4):
+        for q in (0, 2, 1, 3):
             nc.sync.dma_start(
                 out=scale_table[32 * q : 32 * q + 4, :].bitcast(I32),
                 in_=x_scales[0, 4 * q : 4 * q + 4, :].bitcast(I32),

@@ -14,16 +14,20 @@ U8 = mybir.dt.uint8
 FP8X4 = mybir.dt.float8_e4m3fn_x4
 FP4X4 = mybir.dt.float4_e2m1fn_x4
 SILU = mybir.ActivationFunctionType.Silu
+COPY = mybir.ActivationFunctionType.Copy
 MULT = mybir.AluOpType.mult
 
 P = 128
 PACK = 4
 PER_COL = 16
-GATHER = 512
 CHUNK = 128
 GROUP = 256
-SCATTER = 512
 HALF = H // 2
+LATER_AT = 0
+FIRST_AT = 12288
+GROUPED_AT = {"w1": 16384, "w3": 21504}
+GATE_AT = 16896
+ACT_BYTES = 2048
 
 
 def tile_picked_route2_glusilu_p_kernel(
@@ -32,19 +36,22 @@ def tile_picked_route2_glusilu_p_kernel(
     nc = tc.nc
     with ExitStack() as ctx:
         keep = ctx.enter_context(tc.tile_pool(name="keep", bufs=1))
-        stage = ctx.enter_context(tc.tile_pool(name="stage", bufs=1))
+        laid = ctx.enter_context(tc.tile_pool(name="laid", bufs=1))
         psum = ctx.enter_context(tc.psum_pool(name="psum", bufs=1))
+
+        def lay(shape, dtype, name, offset):
+            return laid.tile(shape, dtype, name=name, offset=offset, align_bytes=64)
 
         offs_sb = keep.tile([P, S // PER_COL], U16, name="offs_sb")
         dst_sb = keep.tile([P, S // PER_COL], U16, name="dst_sb")
         word_table = keep.tile([P, T], U16, name="word_table", align_bytes=64)
         scale_table = keep.tile([P, T], U8, name="scale_table", align_bytes=64)
         window = keep.tile([P, U], F32, name="window", align_bytes=64)
-        warm = stage.tile([P, 8], F32, name="warm", tag="slot2", align_bytes=64)
+        zeros = lay([P, 8], F32, "zeros", LATER_AT)
 
-        nc.vector.memset(warm[:], 0.0)
+        nc.vector.memset(zeros[:], 0.0)
         nc.vector.memset(scale_table[:].bitcast(I32), 0)
-        nc.scalar.activation(window[:, 0:8], warm[:], SILU)
+        nc.scalar.activation(window[:, 0:8], zeros[:], SILU)
         nc.vector.memset(window[:, 8:U], 0.0)
 
         nc.sync.dma_start(offs_sb[:], offs)
@@ -55,13 +62,14 @@ def tile_picked_route2_glusilu_p_kernel(
                 out=scale_table[32 * q : 32 * q + 4, :].bitcast(I32),
                 in_=x_scales[0, 4 * q : 4 * q + 4, :].bitcast(I32),
             )
+
         def load_half(tile, w, u):
             nc.sync.dma_start(
                 out=tile, in_=w[:, u * HALF : (u + 1) * HALF].rearrange("(p j) c -> p j c", j=PACK)
             )
 
-        first_raw = stage.tile([P, PACK, HALF], F32, name="first_raw", tag="slot0", align_bytes=64)
-        later_raw = stage.tile([P, 3, PACK, HALF], F32, name="later_raw", tag="slot2", align_bytes=64)
+        first_raw = lay([P, PACK, HALF], F32, "first_raw", FIRST_AT)
+        later_raw = lay([P, 3, PACK, HALF], F32, "later_raw", LATER_AT)
         raw = {("w1", 0): first_raw[:], ("w1", 1): later_raw[:, 0], ("w3", 0): later_raw[:, 1], ("w3", 1): later_raw[:, 2]}
         for name, w in (("w1", w1), ("w3", w3)):
             for u in range(2):
@@ -79,30 +87,32 @@ def tile_picked_route2_glusilu_p_kernel(
             for i, c in enumerate(chunks):
                 x_codes[c] = tile[:, i * CHUNK : (i + 1) * CHUNK]
 
-        def pick_bytes(chunks, tag):
-            tile = stage.tile([P, len(chunks) * CHUNK], U8, name=f"x_bytes{chunks[0]}", tag=tag, align_bytes=64)
+        def pick_bytes(chunks, tile):
             pick(scale_table, tile, chunks[0] * CHUNK, len(chunks) * CHUNK)
             for i, c in enumerate(chunks):
                 x_bytes[c] = tile[:, i * CHUNK : (i + 1) * CHUNK]
 
         pick_words(range(0, 4))
         pick_words(range(4, 8))
-        pick_bytes(range(0, 3), "bytes_first")
-        pick_bytes(range(6, 8), "bytes_last")
+        pick_bytes(range(0, 4), keep.tile([P, 4 * CHUNK], U8, name="bytes_first", align_bytes=64))
+
+        w2_codes = keep.tile([P, N], U32, name="w2_codes", align_bytes=64)
+        w2_scales = keep.tile([P, N], U8, name="w2_scales", align_bytes=64)
+        w2_grouped = keep.tile([P, N, PACK], BF16, name="w2_grouped", align_bytes=64)
 
         codes, scales = {}, {}
         for name in ("w1", "w3"):
-            grouped = stage.tile([P, PACK, P, PACK], BF16, name=f"{name}_grouped", tag=f"{name}_grouped", align_bytes=64)
+            grouped = lay([P, PACK, P, PACK], BF16, f"{name}_grouped", GROUPED_AT[name])
             for u in range(2):
                 src = raw[name, u].rearrange("p j (m t) -> p m j t", t=PACK)
                 dstv = grouped[:, :, 64 * u : 64 * (u + 1), :].rearrange("p t m j -> p m j t")
                 for t in (0, 2):
-                    if name == "w3" and u == 1:
+                    if name == "w3" and u == 1 and t == 0:
                         nc.vector.tensor_copy(dstv[:, :, :, t : t + 2], src[:, :, :, t : t + 2])
                     else:
                         nc.scalar.copy(dstv[:, :, :, t : t + 2], src[:, :, :, t : t + 2])
                 if name == "w1" and u == 0:
-                    w2_raw = stage.tile([P, PACK, N], F32, name="w2_raw", tag="slot0", align_bytes=64)
+                    w2_raw = lay([P, PACK, N], F32, "w2_raw", FIRST_AT)
                     nc.sync.dma_start(out=w2_raw[:], in_=w2.rearrange("(p j) c -> p j c", j=PACK))
             codes[name] = keep.tile([P, H], U32, name=f"{name}_codes", align_bytes=64)
             scales[name] = keep.tile([P, H], U8, name=f"{name}_scales", align_bytes=64)
@@ -112,16 +122,15 @@ def tile_picked_route2_glusilu_p_kernel(
                     scales=scales[name][:, t * P : (t + 2) * P],
                     in_=grouped[:, t : t + 2].rearrange("p t m j -> p (t m j)"),
                 )
+            if name == "w1":
+                pick_bytes(range(4, 6), lay([P, 2 * CHUNK], U8, "bytes_mid", GROUPED_AT["w1"]))
 
-        gate_sb = stage.tile([P, S], F32, name="gate_sb", tag="w1_grouped", align_bytes=64)
+        gate_sb = lay([P, S], F32, "gate_sb", GATE_AT)
         nc.sync.dma_start(out=gate_sb[:], in_=gate)
-        pick_bytes(range(3, 6), "slot2")
-
-        w2_codes = keep.tile([P, N], U32, name="w2_codes", align_bytes=64)
-        w2_scales = keep.tile([P, N], U8, name="w2_scales", align_bytes=64)
+        pick_bytes(range(6, 8), lay([P, 2 * CHUNK], U8, "bytes_last", GROUPED_AT["w3"]))
 
         def product(name, c):
-            tag = f"a{c % 3}" if name == "w1" else f"b{c % 5}"
+            tag = f"bank{c % 5}" if name == "w1" else f"bank{5 + c % 3}"
             bank = psum.tile([P, PACK, CHUNK], F32, name=f"{name}_bank{c}", tag=tag)
             for t in range(PACK):
                 nc.tensor.matmul_mx(
@@ -136,13 +145,25 @@ def tile_picked_route2_glusilu_p_kernel(
             return bank[:].rearrange("p t n -> p n t")
 
         h = [keep.tile([P, GROUP, PACK], BF16, name=f"h{g}", align_bytes=64) for g in range(S // GROUP)]
-        h_mx = []
+        y = {}
+
+        acts = {}
+
+        def activate(c):
+            a = product("w1", c)
+            if c < 5:
+                act = lay([P, CHUNK, PACK], F32, f"act{c}", LATER_AT + (c + 1) * ACT_BYTES)
+            else:
+                act = keep.tile([P, CHUNK, PACK], F32, name=f"act{c}", align_bytes=64)
+            if c == 6:
+                nc.scalar.activation(act[:], a, SILU, bias=window[:, 0:1])
+            else:
+                nc.scalar.activation(act[:], a, SILU)
+            acts[c] = act
 
         def hidden(c):
             g, i = divmod(c, GROUP // CHUNK)
-            a = product("w1", c)
-            act = stage.tile([P, CHUNK, PACK], F32, name=f"act{c}", tag=f"act{c}", align_bytes=64)
-            nc.scalar.activation(act[:], a, SILU)
+            act = acts[c]
             b = product("w3", c)
             nc.vector.tensor_tensor(h[g][:, i * CHUNK : (i + 1) * CHUNK, :], b, act[:], MULT)
 
@@ -154,46 +175,57 @@ def tile_picked_route2_glusilu_p_kernel(
                 scales=h_scales[:],
                 in_=h[g][:].rearrange("p n t -> p (n t)"),
             )
-            h_mx.append((h_codes, h_scales))
+            y[g] = psum.tile([P, GROUP], F32, name=f"y{g}", tag=f"bank{3 + g % 2}")
+            nc.tensor.matmul_mx(
+                out=y[g][:],
+                lhsT=w2_codes[:].bitcast(FP8X4),
+                lhsT_scale=w2_scales[:],
+                rhs=h_codes[:].bitcast(FP8X4),
+                rhs_scale=h_scales[:],
+                start=True,
+                stop=True,
+            )
+
+        weighted = {}
+
+        def weigh(g):
+            weighted[g] = keep.tile([P, GROUP], F32, name=f"weighted{g}", align_bytes=64)
+            nc.vector.tensor_tensor(weighted[g][:], y[g][:], gate_sb[:, g * GROUP : (g + 1) * GROUP], MULT)
+
+        def place(g):
+            cols = slice(g * GROUP // PER_COL, (g + 1) * GROUP // PER_COL)
+            nc.scalar.activation(window[:].indirect(dst_sb[:, cols]), weighted[g][:], COPY)
 
         for c in range(8):
-            hidden(c)
+            activate(c)
             if c == 1:
-                w2_grouped = stage.tile([P, N, PACK], BF16, name="w2_grouped", tag="act0", align_bytes=64)
                 nc.scalar.copy(
                     w2_grouped[:].rearrange("p (c i) j -> p c j i", i=4),
                     w2_raw[:].rearrange("p j (c i) -> p c j i", i=4),
                 )
-            if c == 3:
-                nc.vector.quantize_mx(
-                    out=w2_codes[:].bitcast(FP8X4),
-                    scales=w2_scales[:],
-                    in_=w2_grouped[:].rearrange("p n j -> p (n j)"),
-                )
-            if c in (2, 4):
-                second(c // 2 - 1)
+        hidden(0)
+        hidden(1)
+        nc.vector.quantize_mx(
+            out=w2_codes[:].bitcast(FP8X4),
+            scales=w2_scales[:],
+            in_=w2_grouped[:].rearrange("p n j -> p (n j)"),
+        )
+        second(0)
+        hidden(2)
+        weigh(0)
+        hidden(3)
+        second(1)
+        hidden(4)
+        weigh(1)
+        hidden(5)
         second(2)
+        hidden(6)
+        weigh(2)
+        hidden(7)
         second(3)
-
-        for s in range(S // SCATTER):
-            y = psum.tile([P, SCATTER], F32, name=f"y{s}", tag=f"b{s}")
-            for i in range(SCATTER // GROUP):
-                h_codes, h_scales = h_mx[s * (SCATTER // GROUP) + i]
-                nc.tensor.matmul_mx(
-                    out=y[:, i * GROUP : (i + 1) * GROUP],
-                    lhsT=w2_codes[:].bitcast(FP8X4),
-                    lhsT_scale=w2_scales[:],
-                    rhs=h_codes[:].bitcast(FP8X4),
-                    rhs_scale=h_scales[:],
-                    start=True,
-                    stop=True,
-                )
-            y_sb = stage.tile([P, SCATTER], F32, name=f"y_sb{s}", tag=f"act{6 + s}", align_bytes=64)
-            nc.scalar.copy(y_sb[:], y[:])
-            cols = slice(s * SCATTER // PER_COL, (s + 1) * SCATTER // PER_COL)
-            nc.vector.tensor_tensor(
-                window[:].indirect(dst_sb[:, cols]), y_sb[:], gate_sb[:, s * SCATTER : (s + 1) * SCATTER], MULT
-            )
+        weigh(3)
+        for g in range(4):
+            place(g)
 
         nc.sync.dma_start(out=out[:, 0 : U // 2], in_=window[:, 0 : U // 2])
         nc.scalar.dma_start(out=out[:, U // 2 : U], in_=window[:, U // 2 : U])

@@ -40,22 +40,24 @@ def tile_picked_route2_glusilu_p_kernel(
         psum = ctx.enter_context(tc.psum_pool(name="psum", bufs=1))
 
         def lay(shape, dtype, name, offset):
-            return laid.tile(shape, dtype, name=name, offset=offset, align_bytes=64)
+            return laid.tile(shape, dtype, name=name, offset=offset, align_bytes=256)
 
         offs_sb = keep.tile([P, S // PER_COL], U16, name="offs_sb")
         dst_sb = keep.tile([P, S // PER_COL], U16, name="dst_sb")
-        word_table = keep.tile([P, T], U16, name="word_table", align_bytes=64)
-        scale_table = keep.tile([P, T], U8, name="scale_table", align_bytes=64)
-        window = keep.tile([P, U], F32, name="window", align_bytes=64)
+        word_table = keep.tile([P, T], U16, name="word_table", align_bytes=256)
+        scale_table = keep.tile([P, T], U8, name="scale_table", align_bytes=256)
+        window = keep.tile([P, U], F32, name="window", align_bytes=256)
         zeros = lay([P, 8], F32, "zeros", LATER_AT)
 
+        first_raw = lay([P, PACK, HALF], F32, "first_raw", FIRST_AT)
+        nc.scalar.dma_start(out=word_table[:].bitcast(I32), in_=x_words[0].bitcast(I32))
+        nc.scalar.dma_start(out=first_raw[:], in_=w1[:, 0:HALF].rearrange("(p j) c -> p j c", j=PACK))
         nc.vector.memset(zeros[:], 0.0)
         nc.vector.memset(scale_table[:].bitcast(I32), 0)
         nc.scalar.activation(window[:, 0:8], zeros[:], SILU)
         nc.vector.memset(window[:, 8:U], 0.0)
 
         nc.sync.dma_start(offs_sb[:], offs)
-        nc.sync.dma_start(out=word_table[:].bitcast(I32), in_=x_words[0].bitcast(I32))
         nc.sync.dma_start(dst_sb[:], dst)
         for q in (0, 2, 1, 3):
             nc.sync.dma_start(
@@ -68,12 +70,11 @@ def tile_picked_route2_glusilu_p_kernel(
                 out=tile, in_=w[:, u * HALF : (u + 1) * HALF].rearrange("(p j) c -> p j c", j=PACK)
             )
 
-        first_raw = lay([P, PACK, HALF], F32, "first_raw", FIRST_AT)
         later_raw = lay([P, 3, PACK, HALF], F32, "later_raw", LATER_AT)
         raw = {("w1", 0): first_raw[:], ("w1", 1): later_raw[:, 0], ("w3", 0): later_raw[:, 1], ("w3", 1): later_raw[:, 2]}
-        for name, w in (("w1", w1), ("w3", w3)):
-            for u in range(2):
-                load_half(raw[name, u], w, u)
+        load_half(raw["w1", 1], w1, 1)
+        load_half(raw["w3", 0], w3, 0)
+        load_half(raw["w3", 1], w3, 1)
 
         def pick(table, tile, first, count):
             cols = slice(first // PER_COL, (first + count) // PER_COL)
@@ -82,7 +83,7 @@ def tile_picked_route2_glusilu_p_kernel(
         x_codes, x_bytes = {}, {}
 
         def pick_words(chunks):
-            tile = keep.tile([P, len(chunks) * CHUNK], U16, name=f"x_codes{chunks[0]}", align_bytes=64)
+            tile = keep.tile([P, len(chunks) * CHUNK], U16, name=f"x_codes{chunks[0]}", align_bytes=256)
             pick(word_table, tile, chunks[0] * CHUNK, len(chunks) * CHUNK)
             for i, c in enumerate(chunks):
                 x_codes[c] = tile[:, i * CHUNK : (i + 1) * CHUNK]
@@ -94,11 +95,11 @@ def tile_picked_route2_glusilu_p_kernel(
 
         pick_words(range(0, 4))
         pick_words(range(4, 8))
-        pick_bytes(range(0, 4), keep.tile([P, 4 * CHUNK], U8, name="bytes_first", align_bytes=64))
+        pick_bytes(range(0, 4), keep.tile([P, 4 * CHUNK], U8, name="bytes_first", align_bytes=256))
 
-        w2_codes = keep.tile([P, N], U32, name="w2_codes", align_bytes=64)
-        w2_scales = keep.tile([P, N], U8, name="w2_scales", align_bytes=64)
-        w2_grouped = keep.tile([P, N, PACK], BF16, name="w2_grouped", align_bytes=64)
+        w2_codes = keep.tile([P, N], U32, name="w2_codes", align_bytes=256)
+        w2_scales = keep.tile([P, N], U8, name="w2_scales", align_bytes=256)
+        w2_grouped = keep.tile([P, N, PACK], BF16, name="w2_grouped", align_bytes=256)
 
         codes, scales = {}, {}
         for name in ("w1", "w3"):
@@ -114,8 +115,8 @@ def tile_picked_route2_glusilu_p_kernel(
                 if name == "w1" and u == 0:
                     w2_raw = lay([P, PACK, N], F32, "w2_raw", FIRST_AT)
                     nc.sync.dma_start(out=w2_raw[:], in_=w2.rearrange("(p j) c -> p j c", j=PACK))
-            codes[name] = keep.tile([P, H], U32, name=f"{name}_codes", align_bytes=64)
-            scales[name] = keep.tile([P, H], U8, name=f"{name}_scales", align_bytes=64)
+            codes[name] = keep.tile([P, H], U32, name=f"{name}_codes", align_bytes=256)
+            scales[name] = keep.tile([P, H], U8, name=f"{name}_scales", align_bytes=256)
             for t in (0, 2):
                 nc.vector.quantize_mx(
                     out=codes[name][:, t * P : (t + 2) * P].bitcast(FP8X4),
@@ -144,7 +145,7 @@ def tile_picked_route2_glusilu_p_kernel(
                 )
             return bank[:].rearrange("p t n -> p n t")
 
-        h = [keep.tile([P, GROUP, PACK], BF16, name=f"h{g}", align_bytes=64) for g in range(S // GROUP)]
+        h = [keep.tile([P, GROUP, PACK], BF16, name=f"h{g}", align_bytes=256) for g in range(S // GROUP)]
         y = {}
 
         acts = {}
@@ -154,7 +155,7 @@ def tile_picked_route2_glusilu_p_kernel(
             if c < 5:
                 act = lay([P, CHUNK, PACK], F32, f"act{c}", LATER_AT + (c + 1) * ACT_BYTES)
             else:
-                act = keep.tile([P, CHUNK, PACK], F32, name=f"act{c}", align_bytes=64)
+                act = keep.tile([P, CHUNK, PACK], F32, name=f"act{c}", align_bytes=256)
             if c == 6:
                 nc.scalar.activation(act[:], a, SILU, bias=window[:, 0:1])
             else:
@@ -168,8 +169,8 @@ def tile_picked_route2_glusilu_p_kernel(
             nc.vector.tensor_tensor(h[g][:, i * CHUNK : (i + 1) * CHUNK, :], b, act[:], MULT)
 
         def second(g):
-            h_codes = keep.tile([P, GROUP], U32, name=f"h_codes{g}", align_bytes=64)
-            h_scales = keep.tile([P, GROUP], U8, name=f"h_scales{g}", align_bytes=64)
+            h_codes = keep.tile([P, GROUP], U32, name=f"h_codes{g}", align_bytes=256)
+            h_scales = keep.tile([P, GROUP], U8, name=f"h_scales{g}", align_bytes=256)
             nc.vector.quantize_mx(
                 out=h_codes[:].bitcast(FP8X4),
                 scales=h_scales[:],
@@ -189,7 +190,7 @@ def tile_picked_route2_glusilu_p_kernel(
         weighted = {}
 
         def weigh(g):
-            weighted[g] = keep.tile([P, GROUP], F32, name=f"weighted{g}", align_bytes=64)
+            weighted[g] = keep.tile([P, GROUP], F32, name=f"weighted{g}", align_bytes=256)
             nc.vector.tensor_tensor(weighted[g][:], y[g][:], gate_sb[:, g * GROUP : (g + 1) * GROUP], MULT)
 
         def place(g):

@@ -131,7 +131,7 @@ def tile_picked_route2_glusilu_p_kernel(
         pick_bytes(range(6, 8), lay([P, 2 * CHUNK], U8, "bytes_last", GROUPED_AT["w3"]))
 
         def product(name, c):
-            tag = f"bank{c % 5}" if name == "w1" else f"bank{5 + c % 3}"
+            tag = f"bank{c % 3}" if name == "w1" else f"bank{5 + c % 3}"
             bank = psum.tile([P, PACK, CHUNK], F32, name=f"{name}_bank{c}", tag=tag)
             for t in range(PACK):
                 nc.tensor.matmul_mx(
@@ -153,7 +153,7 @@ def tile_picked_route2_glusilu_p_kernel(
         def activate(c):
             a = product("w1", c)
             if c < 5:
-                act = lay([P, CHUNK, PACK], F32, f"act{c}", LATER_AT + (c + 1) * ACT_BYTES)
+                act = lay([P, CHUNK, PACK], F32, f"act{c}", LATER_AT + ((c + 3) % 5 + 1) * ACT_BYTES)
             else:
                 act = keep.tile([P, CHUNK, PACK], F32, name=f"act{c}", align_bytes=256)
             if c == 6:
@@ -162,11 +162,15 @@ def tile_picked_route2_glusilu_p_kernel(
                 nc.scalar.activation(act[:], a, SILU)
             acts[c] = act
 
+        ups = {}
+
+        def up(c):
+            ups[c] = product("w3", c)
+
         def hidden(c):
             g, i = divmod(c, GROUP // CHUNK)
             act = acts[c]
-            b = product("w3", c)
-            nc.vector.tensor_tensor(h[g][:, i * CHUNK : (i + 1) * CHUNK, :], b, act[:], MULT)
+            nc.vector.tensor_tensor(h[g][:, i * CHUNK : (i + 1) * CHUNK, :], ups[c], act[:], MULT)
 
         def second(g):
             h_codes = keep.tile([P, GROUP], U32, name=f"h_codes{g}", align_bytes=256)
@@ -197,13 +201,18 @@ def tile_picked_route2_glusilu_p_kernel(
             cols = slice(g * GROUP // PER_COL, (g + 1) * GROUP // PER_COL)
             nc.scalar.activation(window[:].indirect(dst_sb[:, cols]), weighted[g][:], COPY)
 
-        for c in range(8):
+        for c in range(3):
             activate(c)
-            if c == 1:
-                nc.scalar.copy(
-                    w2_grouped[:].rearrange("p (c i) j -> p c j i", i=4),
-                    w2_raw[:].rearrange("p j (c i) -> p c j i", i=4),
-                )
+        nc.scalar.copy(
+            w2_grouped[:].rearrange("p (c i) j -> p c j i", i=4),
+            w2_raw[:].rearrange("p j (c i) -> p c j i", i=4),
+        )
+        up(0)
+        activate(3)
+        up(1)
+        activate(4)
+        up(2)
+        activate(5)
         hidden(0)
         hidden(1)
         nc.vector.quantize_mx(
@@ -211,20 +220,21 @@ def tile_picked_route2_glusilu_p_kernel(
             scales=w2_scales[:],
             in_=w2_grouped[:].rearrange("p n j -> p (n j)"),
         )
+        activate(6)
         second(0)
+        up(3)
+        activate(7)
         hidden(2)
         weigh(0)
-        hidden(3)
-        second(1)
-        hidden(4)
-        weigh(1)
-        hidden(5)
-        second(2)
-        hidden(6)
-        weigh(2)
-        hidden(7)
-        second(3)
-        weigh(3)
+        for g in range(1, 4):
+            if g < 3:
+                up(2 * g + 2)
+            hidden(2 * g + 1)
+            second(g)
+            if g < 3:
+                up(2 * g + 3)
+                hidden(2 * g + 2)
+            weigh(g)
         for g in range(4):
             place(g)
 

@@ -131,7 +131,7 @@ def tile_picked_route2_glusilu_p_kernel(
         pick_bytes(range(6, 8), lay([P, 2 * CHUNK], U8, "bytes_last", GROUPED_AT["w3"]))
 
         def product(name, c):
-            tag = f"bank{c % 3}" if name == "w1" else f"bank{5 + c % 3}"
+            tag = f"bank{c % 4}" if name == "w1" else f"bank{5 + c % 3}"
             bank = psum.tile([P, PACK, CHUNK], F32, name=f"{name}_bank{c}", tag=tag)
             for t in range(PACK):
                 nc.tensor.matmul_mx(
@@ -180,7 +180,7 @@ def tile_picked_route2_glusilu_p_kernel(
                 scales=h_scales[:],
                 in_=h[g][:].rearrange("p n t -> p (n t)"),
             )
-            y[g] = psum.tile([P, GROUP], F32, name=f"y{g}", tag=f"bank{3 + g % 2}")
+            y[g] = psum.tile([P, GROUP], F32, name=f"y{g}", tag="bank4")
             nc.tensor.matmul_mx(
                 out=y[g][:],
                 lhsT=w2_codes[:].bitcast(FP8X4),
@@ -207,8 +207,8 @@ def tile_picked_route2_glusilu_p_kernel(
             w2_grouped[:].rearrange("p (c i) j -> p c j i", i=4),
             w2_raw[:].rearrange("p j (c i) -> p c j i", i=4),
         )
-        up(0)
         activate(3)
+        up(0)
         up(1)
         activate(4)
         up(2)
@@ -221,9 +221,9 @@ def tile_picked_route2_glusilu_p_kernel(
             in_=w2_grouped[:].rearrange("p n j -> p (n j)"),
         )
         activate(6)
+        activate(7)
         second(0)
         up(3)
-        activate(7)
         hidden(2)
         weigh(0)
         for g in range(1, 4):

@@ -23,11 +23,16 @@ PER_COL = 16
 CHUNK = 128
 GROUP = 256
 HALF = H // 2
-LATER_AT = 0
-FIRST_AT = 12288
+SCALE_ROWS = 16
+TOP = P - SCALE_ROWS
+EARLY = 6 * CHUNK
+W1_SECOND_AT = 0
+W3_SECOND_AT = 4096
+H_AT = 12288
 GROUPED_AT = {"w1": 16384, "w3": 21504}
-GATE_AT = 16896
-ACT_BYTES = 2048
+GATE_AT = 17408
+W1_BANK = (0, 1, 2, 3, 0, 1, 2, 6)
+W3_BANK = (4, 5, 4, 5, 4, 5, 4, 5)
 
 
 def tile_picked_route2_glusilu_p_kernel(
@@ -39,99 +44,117 @@ def tile_picked_route2_glusilu_p_kernel(
         laid = ctx.enter_context(tc.tile_pool(name="laid", bufs=1))
         psum = ctx.enter_context(tc.psum_pool(name="psum", bufs=1))
 
-        def lay(shape, dtype, name, offset):
-            return laid.tile(shape, dtype, name=name, offset=offset, align_bytes=256)
-
-        offs_sb = keep.tile([P, S // PER_COL], U16, name="offs_sb")
-        dst_sb = keep.tile([P, S // PER_COL], U16, name="dst_sb")
-        word_table = keep.tile([P, T], U16, name="word_table", align_bytes=256)
-        scale_table = keep.tile([P, T], U8, name="scale_table", align_bytes=256)
-        window = keep.tile([P, U], F32, name="window", align_bytes=256)
-        zeros = lay([P, 8], F32, "zeros", LATER_AT)
-
-        first_raw = lay([P, PACK, HALF], F32, "first_raw", FIRST_AT)
-        nc.scalar.dma_start(out=word_table[:].bitcast(I32), in_=x_words[0].bitcast(I32))
-        nc.scalar.dma_start(out=first_raw[:], in_=w1[:, 0:HALF].rearrange("(p j) c -> p j c", j=PACK))
-        nc.vector.memset(zeros[:], 0.0)
-        nc.vector.memset(scale_table[:].bitcast(I32), 0)
-        nc.scalar.activation(window[:, 0:8], zeros[:], SILU)
-        nc.vector.memset(window[:, 8:U], 0.0)
-
-        nc.sync.dma_start(offs_sb[:], offs)
-        nc.sync.dma_start(dst_sb[:], dst)
-        for q in (0, 2, 1, 3):
-            nc.sync.dma_start(
-                out=scale_table[32 * q : 32 * q + 4, :].bitcast(I32),
-                in_=x_scales[0, 4 * q : 4 * q + 4, :].bitcast(I32),
-            )
+        def lay(shape, dtype, name, offset, align=256):
+            return laid.tile(shape, dtype, name=name, offset=offset, align_bytes=align)
 
         def load_half(tile, w, u):
             nc.sync.dma_start(
                 out=tile, in_=w[:, u * HALF : (u + 1) * HALF].rearrange("(p j) c -> p j c", j=PACK)
             )
 
-        later_raw = lay([P, 3, PACK, HALF], F32, "later_raw", LATER_AT)
-        raw = {("w1", 0): first_raw[:], ("w1", 1): later_raw[:, 0], ("w3", 0): later_raw[:, 1], ("w3", 1): later_raw[:, 2]}
-        load_half(raw["w1", 1], w1, 1)
-        load_half(raw["w3", 0], w3, 0)
-        load_half(raw["w3", 1], w3, 1)
+        offs_sb = keep.tile([P, S // PER_COL], U16, name="offs_sb")
+        dst_sb = keep.tile([P, S // PER_COL], U16, name="dst_sb")
+        word_table = keep.tile([P, T], U16, name="word_table", align_bytes=256)
+        scale_table = keep.tile([P, T], U8, name="scale_table", align_bytes=256)
+        window = keep.tile([P, U], F32, name="window", align_bytes=256)
+        zeros = keep.tile([P, 8], F32, name="zeros")
+        w1_first = keep.tile([P, PACK, HALF], F32, name="w1_first", align_bytes=256)
+        w1_second = lay([P, PACK, HALF], F32, "w1_second", W1_SECOND_AT)
+        w3_first = keep.tile([P, PACK, HALF], F32, name="w3_first", align_bytes=256)
+        w3_room = lay([P, 2, PACK, HALF], F32, "w3_room", W3_SECOND_AT)
+        spans = ((0, EARLY), (EARLY, S - EARLY))
+        picked = [keep.tile([P, n], U8, name=f"picked{at}", align_bytes=256) for at, n in spans]
+        placed = [keep.tile([P, n], U8, name=f"placed{at}", align_bytes=256) for at, n in spans]
+
+        nc.sync.dma_start(offs_sb[:], offs)
+        nc.sync.dma_start(out=scale_table[TOP:P, :].bitcast(I32), in_=x_scales[0].bitcast(I32))
+        nc.sync.dma_start(out=word_table[:].bitcast(I32), in_=x_words[0].bitcast(I32))
+        load_half(w1_first[:], w1, 0)
+        load_half(w1_second[:], w1, 1)
+        load_half(w3_first[:], w3, 0)
+
+        nc.vector.memset(zeros[:], 0.0)
+        nc.vector.memset(scale_table[0:TOP, :].bitcast(I32), 0)
+        for tile in placed:
+            nc.vector.memset(tile[:].bitcast(I32), 0)
+        nc.scalar.activation(window[:], zeros[:, 0:1].to_broadcast([P, U]), SILU)
 
         def pick(table, tile, first, count):
             cols = slice(first // PER_COL, (first + count) // PER_COL)
             nc.vector.tensor_copy(tile[:], table[:].indirect(offs_sb[:, cols]))
 
-        x_codes, x_bytes = {}, {}
+        x_codes = {}
 
-        def pick_words(chunks):
-            tile = keep.tile([P, len(chunks) * CHUNK], U16, name=f"x_codes{chunks[0]}", align_bytes=256)
+        def pick_words(chunks, tile):
             pick(word_table, tile, chunks[0] * CHUNK, len(chunks) * CHUNK)
             for i, c in enumerate(chunks):
                 x_codes[c] = tile[:, i * CHUNK : (i + 1) * CHUNK]
 
-        def pick_bytes(chunks, tile):
-            pick(scale_table, tile, chunks[0] * CHUNK, len(chunks) * CHUNK)
-            for i, c in enumerate(chunks):
-                x_bytes[c] = tile[:, i * CHUNK : (i + 1) * CHUNK]
+        def move_rows(u):
+            for q in (0, 2, 1, 3):
+                nc.sync.dma_start(
+                    out=placed[u][32 * q : 32 * q + 4, :].bitcast(I32),
+                    in_=picked[u][TOP + 4 * q : TOP + 4 * q + 4, :].bitcast(I32),
+                )
 
-        pick_words(range(0, 4))
-        pick_words(range(4, 8))
-        pick_bytes(range(0, 4), keep.tile([P, 4 * CHUNK], U8, name="bytes_first", align_bytes=256))
+        pick(scale_table, picked[0], *spans[0])
+        move_rows(0)
+        load_half(w3_room[:, 0], w3, 1)
+        pick(scale_table, picked[1], *spans[1])
+        move_rows(1)
+        nc.sync.dma_start(dst_sb[:], dst)
+        pick_words(range(0, 4), keep.tile([P, 4 * CHUNK], U16, name="words_first", align_bytes=256))
+        x_bytes = {}
+        for c in range(S // CHUNK):
+            u = int(c * CHUNK >= EARLY)
+            x_bytes[c] = placed[u][:, c * CHUNK - spans[u][0] : (c + 1) * CHUNK - spans[u][0]]
 
-        w2_codes = keep.tile([P, N], U32, name="w2_codes", align_bytes=256)
-        w2_scales = keep.tile([P, N], U8, name="w2_scales", align_bytes=256)
-        w2_grouped = keep.tile([P, N, PACK], BF16, name="w2_grouped", align_bytes=256)
-
-        codes, scales = {}, {}
+        raw = {("w1", 0): w1_first[:], ("w1", 1): w1_second[:], ("w3", 0): w3_first[:], ("w3", 1): w3_room[:, 0]}
+        grouped, codes, scales = {}, {}, {}
         for name in ("w1", "w3"):
-            grouped = lay([P, PACK, P, PACK], BF16, f"{name}_grouped", GROUPED_AT[name])
-            for u in range(2):
-                src = raw[name, u].rearrange("p j (m t) -> p m j t", t=PACK)
-                dstv = grouped[:, :, 64 * u : 64 * (u + 1), :].rearrange("p t m j -> p m j t")
-                for t in (0, 2):
-                    if name == "w3" and u == 1 and t == 0:
-                        nc.vector.tensor_copy(dstv[:, :, :, t : t + 2], src[:, :, :, t : t + 2])
-                    else:
-                        nc.scalar.copy(dstv[:, :, :, t : t + 2], src[:, :, :, t : t + 2])
-                if name == "w1" and u == 0:
-                    w2_raw = lay([P, PACK, N], F32, "w2_raw", FIRST_AT)
-                    nc.sync.dma_start(out=w2_raw[:], in_=w2.rearrange("(p j) c -> p j c", j=PACK))
+            grouped[name] = lay([P, PACK, P, PACK], BF16, f"{name}_grouped", GROUPED_AT[name])
             codes[name] = keep.tile([P, H], U32, name=f"{name}_codes", align_bytes=256)
             scales[name] = keep.tile([P, H], U8, name=f"{name}_scales", align_bytes=256)
+
+        def cast(name, u, t, on_vector):
+            src = raw[name, u].rearrange("p j (m t) -> p m j t", t=PACK)[:, :, :, t : t + 2]
+            to = grouped[name][:, :, 64 * u : 64 * (u + 1), :].rearrange("p t m j -> p m j t")[:, :, :, t : t + 2]
+            if on_vector:
+                nc.vector.tensor_copy(to, src)
+            else:
+                nc.scalar.copy(to, src)
+
+        def quantise(name):
             for t in (0, 2):
                 nc.vector.quantize_mx(
                     out=codes[name][:, t * P : (t + 2) * P].bitcast(FP8X4),
                     scales=scales[name][:, t * P : (t + 2) * P],
-                    in_=grouped[:, t : t + 2].rearrange("p t m j -> p (t m j)"),
+                    in_=grouped[name][:, t : t + 2].rearrange("p t m j -> p (t m j)"),
                 )
-            if name == "w1":
-                pick_bytes(range(4, 6), lay([P, 2 * CHUNK], U8, "bytes_mid", GROUPED_AT["w1"]))
 
+        cast("w1", 0, 0, False)
+        cast("w1", 0, 2, False)
+        cast("w1", 1, 0, True)
+        cast("w1", 1, 2, False)
+        w2_raw = lay([P, PACK, N], F32, "w2_raw", W1_SECOND_AT)
+        nc.scalar.dma_start(out=w2_raw[:], in_=w2.rearrange("(p j) c -> p j c", j=PACK))
+        quantise("w1")
+        pick_words(range(6, 8), lay([P, 2 * CHUNK], U16, "words_mid", GROUPED_AT["w1"]))
         gate_sb = lay([P, S], F32, "gate_sb", GATE_AT)
         nc.sync.dma_start(out=gate_sb[:], in_=gate)
-        pick_bytes(range(6, 8), lay([P, 2 * CHUNK], U8, "bytes_last", GROUPED_AT["w3"]))
+        cast("w3", 0, 0, False)
+        cast("w3", 0, 2, False)
+        cast("w3", 1, 0, True)
+        cast("w3", 1, 2, True)
+        quantise("w3")
+        pick_words(range(4, 6), lay([P, 2 * CHUNK], U16, "words_last", GROUPED_AT["w3"]))
+
+        w2_codes = keep.tile([P, N], U32, name="w2_codes", align_bytes=256)
+        w2_scales = keep.tile([P, N], U8, name="w2_scales", align_bytes=256)
+        w2_grouped = lay([P, N, PACK], BF16, "w2_grouped", W3_SECOND_AT)
 
         def product(name, c):
-            tag = f"bank{c % 4}" if name == "w1" else f"bank{5 + c % 3}"
+            tag = f"bank{(W1_BANK if name == 'w1' else W3_BANK)[c]}"
             bank = psum.tile([P, PACK, CHUNK], F32, name=f"{name}_bank{c}", tag=tag)
             for t in range(PACK):
                 nc.tensor.matmul_mx(
@@ -145,53 +168,52 @@ def tile_picked_route2_glusilu_p_kernel(
                 )
             return bank[:].rearrange("p t n -> p n t")
 
-        h = [keep.tile([P, GROUP, PACK], BF16, name=f"h{g}", align_bytes=256) for g in range(S // GROUP)]
-        y = {}
-
-        acts = {}
+        h = {g: keep.tile([P, GROUP, PACK], BF16, name=f"h{g}", align_bytes=256) for g in (2, 3)}
+        h_first = [
+            lay([P, CHUNK, PACK], BF16, "h_first0", H_AT),
+            keep.tile([P, CHUNK, PACK], BF16, name="h_first1", align_bytes=256),
+        ]
+        y, acts, ups, weighted = {}, {}, {}, {}
 
         def activate(c):
             a = product("w1", c)
-            if c < 5:
-                act = lay([P, CHUNK, PACK], F32, f"act{c}", LATER_AT + ((c + 3) % 5 + 1) * ACT_BYTES)
+            if c in (2, 3):
+                acts[c] = lay([P, CHUNK, PACK], F32, f"act{c}", W3_SECOND_AT + (c - 1) * 4 * PACK * CHUNK)
             else:
-                act = keep.tile([P, CHUNK, PACK], F32, name=f"act{c}", align_bytes=256)
+                acts[c] = keep.tile([P, CHUNK, PACK], F32, name=f"act{c}", align_bytes=256)
             if c == 6:
-                nc.scalar.activation(act[:], a, SILU, bias=window[:, 0:1])
+                nc.scalar.activation(acts[c][:], a, SILU, bias=window[:, 0:1])
             else:
-                nc.scalar.activation(act[:], a, SILU)
-            acts[c] = act
-
-        ups = {}
+                nc.scalar.activation(acts[c][:], a, SILU)
 
         def up(c):
             ups[c] = product("w3", c)
 
         def hidden(c):
             g, i = divmod(c, GROUP // CHUNK)
-            act = acts[c]
-            nc.vector.tensor_tensor(h[g][:, i * CHUNK : (i + 1) * CHUNK, :], ups[c], act[:], MULT)
+            to = h_first[i][:] if g == 0 else h[g][:, i * CHUNK : (i + 1) * CHUNK, :]
+            nc.vector.tensor_tensor(to, ups[c], acts[c][:], MULT)
 
         def second(g):
             h_codes = keep.tile([P, GROUP], U32, name=f"h_codes{g}", align_bytes=256)
             h_scales = keep.tile([P, GROUP], U8, name=f"h_scales{g}", align_bytes=256)
-            nc.vector.quantize_mx(
-                out=h_codes[:].bitcast(FP8X4),
-                scales=h_scales[:],
-                in_=h[g][:].rearrange("p n t -> p (n t)"),
-            )
-            y[g] = psum.tile([P, GROUP], F32, name=f"y{g}", tag="bank4")
-            nc.tensor.matmul_mx(
-                out=y[g][:],
-                lhsT=w2_codes[:].bitcast(FP8X4),
-                lhsT_scale=w2_scales[:],
-                rhs=h_codes[:].bitcast(FP8X4),
-                rhs_scale=h_scales[:],
-                start=True,
-                stop=True,
-            )
-
-        weighted = {}
+            y[g] = psum.tile([P, GROUP], F32, name=f"y{g}", tag="bank7")
+            pieces = [(h_first[0][:], 0, CHUNK), (h_first[1][:], CHUNK, GROUP)] if g == 0 else [(h[g][:], 0, GROUP)]
+            for values, a, b in pieces:
+                nc.vector.quantize_mx(
+                    out=h_codes[:, a:b].bitcast(FP8X4),
+                    scales=h_scales[:, a:b],
+                    in_=values.rearrange("p n t -> p (n t)"),
+                )
+                nc.tensor.matmul_mx(
+                    out=y[g][:, a:b],
+                    lhsT=w2_codes[:].bitcast(FP8X4),
+                    lhsT_scale=w2_scales[:],
+                    rhs=h_codes[:, a:b].bitcast(FP8X4),
+                    rhs_scale=h_scales[:, a:b],
+                    start=True,
+                    stop=True,
+                )
 
         def weigh(g):
             weighted[g] = keep.tile([P, GROUP], F32, name=f"weighted{g}", align_bytes=256)
@@ -201,39 +223,37 @@ def tile_picked_route2_glusilu_p_kernel(
             cols = slice(g * GROUP // PER_COL, (g + 1) * GROUP // PER_COL)
             nc.scalar.activation(window[:].indirect(dst_sb[:, cols]), weighted[g][:], COPY)
 
-        for c in range(3):
-            activate(c)
+        activate(0)
+        activate(1)
         nc.scalar.copy(
             w2_grouped[:].rearrange("p (c i) j -> p c j i", i=4),
             w2_raw[:].rearrange("p j (c i) -> p c j i", i=4),
         )
-        activate(3)
-        up(0)
-        up(1)
-        activate(4)
-        up(2)
-        activate(5)
-        hidden(0)
-        hidden(1)
         nc.vector.quantize_mx(
             out=w2_codes[:].bitcast(FP8X4),
             scales=w2_scales[:],
             in_=w2_grouped[:].rearrange("p n j -> p (n j)"),
         )
+        activate(2)
+        activate(3)
+        up(0)
+        up(1)
+        activate(4)
+        activate(5)
+        hidden(0)
+        up(2)
         activate(6)
-        activate(7)
-        second(0)
+        hidden(1)
         up(3)
-        hidden(2)
-        weigh(0)
-        for g in range(1, 4):
-            if g < 3:
-                up(2 * g + 2)
-            hidden(2 * g + 1)
+        for g in range(4):
             second(g)
-            if g < 3:
-                up(2 * g + 3)
-                hidden(2 * g + 2)
+            if g == 0:
+                activate(7)
+                h[1] = lay([P, GROUP, PACK], BF16, "h1", H_AT)
+            for c in range(2 * g + 2, min(2 * g + 4, 8)):
+                hidden(c)
+                if c + 2 < 8:
+                    up(c + 2)
             weigh(g)
         for g in range(4):
             place(g)

@@ -26,11 +26,10 @@ HALF = H // 2
 SCALE_ROWS = 16
 TOP = P - SCALE_ROWS
 EARLY = 6 * CHUNK
-W1_SECOND_AT = 0
 W3_SECOND_AT = 4096
 H_AT = 12288
-GROUPED_AT = {"w1": 16384, "w3": 21504}
-GATE_AT = 17408
+GROUPED_AT = {"w1": 16384, "w3": 22528}
+GATE_AT = 18432
 W1_BANK = (0, 1, 2, 3, 0, 1, 2, 6)
 W3_BANK = (4, 5, 4, 5, 4, 5, 4, 5)
 
@@ -59,7 +58,7 @@ def tile_picked_route2_glusilu_p_kernel(
         window = keep.tile([P, U], F32, name="window", align_bytes=256)
         zeros = keep.tile([P, 8], F32, name="zeros")
         w1_first = keep.tile([P, PACK, HALF], F32, name="w1_first", align_bytes=256)
-        w1_second = lay([P, PACK, HALF], F32, "w1_second", W1_SECOND_AT)
+        w1_second = keep.tile([P, PACK, HALF], F32, name="w1_second", align_bytes=256)
         w3_first = keep.tile([P, PACK, HALF], F32, name="w3_first", align_bytes=256)
         w3_room = lay([P, 2, PACK, HALF], F32, "w3_room", W3_SECOND_AT)
         spans = ((0, EARLY), (EARLY, S - EARLY))
@@ -68,16 +67,17 @@ def tile_picked_route2_glusilu_p_kernel(
 
         nc.sync.dma_start(offs_sb[:], offs)
         nc.sync.dma_start(out=scale_table[TOP:P, :].bitcast(I32), in_=x_scales[0].bitcast(I32))
-        nc.sync.dma_start(out=word_table[:].bitcast(I32), in_=x_words[0].bitcast(I32))
         load_half(w1_first[:], w1, 0)
         load_half(w1_second[:], w1, 1)
+        nc.sync.dma_start(out=word_table[:].bitcast(I32), in_=x_words[0].bitcast(I32))
         load_half(w3_first[:], w3, 0)
 
         nc.vector.memset(zeros[:], 0.0)
         nc.vector.memset(scale_table[0:TOP, :].bitcast(I32), 0)
         for tile in placed:
             nc.vector.memset(tile[:].bitcast(I32), 0)
-        nc.scalar.activation(window[:], zeros[:, 0:1].to_broadcast([P, U]), SILU)
+        nc.scalar.activation(window[:, 0 : U // 2], zeros[:, 0:1].to_broadcast([P, U // 2]), SILU)
+        nc.vector.memset(window[:, U // 2 : U], 0.0)
 
         def pick(table, tile, first, count):
             cols = slice(first // PER_COL, (first + count) // PER_COL)
@@ -103,7 +103,6 @@ def tile_picked_route2_glusilu_p_kernel(
         pick(scale_table, picked[1], *spans[1])
         move_rows(1)
         nc.sync.dma_start(dst_sb[:], dst)
-        pick_words(range(0, 4), keep.tile([P, 4 * CHUNK], U16, name="words_first", align_bytes=256))
         x_bytes = {}
         for c in range(S // CHUNK):
             u = int(c * CHUNK >= EARLY)
@@ -136,10 +135,12 @@ def tile_picked_route2_glusilu_p_kernel(
         cast("w1", 0, 2, False)
         cast("w1", 1, 0, True)
         cast("w1", 1, 2, False)
-        w2_raw = lay([P, PACK, N], F32, "w2_raw", W1_SECOND_AT)
-        nc.scalar.dma_start(out=w2_raw[:], in_=w2.rearrange("(p j) c -> p j c", j=PACK))
         quantise("w1")
-        pick_words(range(6, 8), lay([P, 2 * CHUNK], U16, "words_mid", GROUPED_AT["w1"]))
+        w2_raw = lay([P, PACK, N], F32, "w2_raw", GROUPED_AT["w1"])
+        nc.scalar.dma_start(out=w2_raw[:], in_=w2.rearrange("(p j) c -> p j c", j=PACK))
+        for first in (0, 2, 6):
+            words = keep.tile([P, 2 * CHUNK], U16, name=f"words{first}", align_bytes=256)
+            pick_words(range(first, first + 2), words)
         gate_sb = lay([P, S], F32, "gate_sb", GATE_AT)
         nc.sync.dma_start(out=gate_sb[:], in_=gate)
         cast("w3", 0, 0, False)

@@ -136,6 +136,17 @@ def tile_picked_route2_glusilu_p_kernel(
         cast("w1", 1, 0, True)
         cast("w1", 1, 2, False)
         quantise("w1")
+        warm = psum.tile([P, 2 * GROUP], F32, name="warm", tag="bank7")
+        for i, width in enumerate((GROUP, GROUP, GROUP, CHUNK)):
+            nc.tensor.matmul_mx(
+                out=warm[:, i % 2 * GROUP : i % 2 * GROUP + width],
+                lhsT=codes["w1"][:, 0:P].bitcast(FP8X4),
+                lhsT_scale=scales["w1"][:, 0:P],
+                rhs=codes["w1"][:, 0:width].bitcast(FP8X4),
+                rhs_scale=scales["w1"][:, 0:width],
+                start=True,
+                stop=True,
+            )
         w2_raw = lay([P, PACK, N], F32, "w2_raw", GROUPED_AT["w1"])
         nc.scalar.dma_start(out=w2_raw[:], in_=w2.rearrange("(p j) c -> p j c", j=PACK))
         for first in (0, 2, 6):

@@ -21,17 +21,25 @@ P = 128
 PACK = 4
 PER_COL = 16
 CHUNK = 128
+CHUNKS = S // CHUNK
 GROUP = 256
-HALF = H // 2
+CUTS = {"w1": (0, 256, 512), "w3": (0, 192, 384, 512)}
 SCALE_ROWS = 16
 TOP = P - SCALE_ROWS
 EARLY = 6 * CHUNK
-W3_SECOND_AT = 4096
-H_AT = 12288
-GROUPED_AT = {"w1": 16384, "w3": 22528}
-GATE_AT = 18432
-W1_BANK = (0, 1, 2, 3, 0, 1, 2, 6)
-W3_BANK = (4, 5, 4, 5, 4, 5, 4, 5)
+EVEN_AT = 0
+W1_GROUPED_AT = 18432
+W2_RAW_AT = W1_GROUPED_AT
+ODD_AT = (1024, 2048, 4096, 6144)
+ODD_CODES_AT = (2816, 4864, 6912)
+W3_SECOND_AT = 28672
+ACT_AT = {2: W3_SECOND_AT - 1536, 3: W3_SECOND_AT + 1536, 4: 8704}
+W3_GROUPED_AT = {0: 10240, 2: 13312}
+LAST_WORDS_AT = 11264
+FIRST_WORDS_AT = 17408
+W1_BANK = (0, 1, 2, 3, 4, 2, 3, 4)
+W3_BANK = (6, 7, 0, 1, 0, 1, 0, 1)
+Y_BANK = (6, 7, 5, 2, 6, 3, 5, 2)
 
 
 def tile_picked_route2_glusilu_p_kernel(
@@ -43,34 +51,38 @@ def tile_picked_route2_glusilu_p_kernel(
         laid = ctx.enter_context(tc.tile_pool(name="laid", bufs=1))
         psum = ctx.enter_context(tc.psum_pool(name="psum", bufs=1))
 
-        def lay(shape, dtype, name, offset, align=256):
-            return laid.tile(shape, dtype, name=name, offset=offset, align_bytes=align)
+        def lay(shape, dtype, name, offset):
+            return laid.tile(shape, dtype, name=name, offset=offset, align_bytes=256)
 
-        def load_half(tile, w, u):
-            nc.sync.dma_start(
-                out=tile, in_=w[:, u * HALF : (u + 1) * HALF].rearrange("(p j) c -> p j c", j=PACK)
-            )
+        def own(shape, dtype, name):
+            return keep.tile(shape, dtype, name=name, align_bytes=256)
+
+        raw = {}
+
+        def load_piece(name, w, u):
+            a, b = CUTS[name][u : u + 2]
+            if (name, b) == ("w3", H):
+                raw[name, u] = lay([P, PACK, b - a], F32, "w3_last", W3_SECOND_AT)
+            else:
+                raw[name, u] = own([P, PACK, b - a], F32, f"{name}_raw{u}")
+            nc.sync.dma_start(out=raw[name, u][:], in_=w[:, a:b].rearrange("(p j) c -> p j c", j=PACK))
 
         offs_sb = keep.tile([P, S // PER_COL], U16, name="offs_sb")
         dst_sb = keep.tile([P, S // PER_COL], U16, name="dst_sb")
-        word_table = keep.tile([P, T], U16, name="word_table", align_bytes=256)
-        scale_table = keep.tile([P, T], U8, name="scale_table", align_bytes=256)
-        window = keep.tile([P, U], F32, name="window", align_bytes=256)
+        word_table = own([P, T], U16, "word_table")
+        scale_table = own([P, T], U8, "scale_table")
+        window = own([P, U], F32, "window")
         zeros = keep.tile([P, 8], F32, name="zeros")
-        w1_first = keep.tile([P, PACK, HALF], F32, name="w1_first", align_bytes=256)
-        w1_second = keep.tile([P, PACK, HALF], F32, name="w1_second", align_bytes=256)
-        w3_first = keep.tile([P, PACK, HALF], F32, name="w3_first", align_bytes=256)
-        w3_room = lay([P, 2, PACK, HALF], F32, "w3_room", W3_SECOND_AT)
         spans = ((0, EARLY), (EARLY, S - EARLY))
-        picked = [keep.tile([P, n], U8, name=f"picked{at}", align_bytes=256) for at, n in spans]
-        placed = [keep.tile([P, n], U8, name=f"placed{at}", align_bytes=256) for at, n in spans]
+        picked = [own([P, n], U8, f"picked{at}") for at, n in spans]
+        placed = [own([P, n], U8, f"placed{at}") for at, n in spans]
 
         nc.sync.dma_start(offs_sb[:], offs)
         nc.sync.dma_start(out=scale_table[TOP:P, :].bitcast(I32), in_=x_scales[0].bitcast(I32))
-        load_half(w1_first[:], w1, 0)
-        load_half(w1_second[:], w1, 1)
+        load_piece("w1", w1, 0)
+        load_piece("w1", w1, 1)
         nc.sync.dma_start(out=word_table[:].bitcast(I32), in_=x_words[0].bitcast(I32))
-        load_half(w3_first[:], w3, 0)
+        load_piece("w3", w3, 0)
 
         nc.vector.memset(zeros[:], 0.0)
         nc.vector.memset(scale_table[0:TOP, :].bitcast(I32), 0)
@@ -83,13 +95,6 @@ def tile_picked_route2_glusilu_p_kernel(
             cols = slice(first // PER_COL, (first + count) // PER_COL)
             nc.vector.tensor_copy(tile[:], table[:].indirect(offs_sb[:, cols]))
 
-        x_codes = {}
-
-        def pick_words(chunks, tile):
-            pick(word_table, tile, chunks[0] * CHUNK, len(chunks) * CHUNK)
-            for i, c in enumerate(chunks):
-                x_codes[c] = tile[:, i * CHUNK : (i + 1) * CHUNK]
-
         def move_rows(u):
             for q in (0, 2, 1, 3):
                 nc.sync.dma_start(
@@ -99,25 +104,35 @@ def tile_picked_route2_glusilu_p_kernel(
 
         pick(scale_table, picked[0], *spans[0])
         move_rows(0)
-        load_half(w3_room[:, 0], w3, 1)
+        load_piece("w3", w3, 1)
+        load_piece("w3", w3, 2)
         pick(scale_table, picked[1], *spans[1])
         move_rows(1)
+        gate_first = own([P, GROUP], F32, "gate_first")
+        nc.sync.dma_start(out=gate_first[:], in_=gate[:, 0:GROUP])
+        gate_rest = own([P, S - GROUP], F32, "gate_rest")
         nc.sync.dma_start(dst_sb[:], dst)
+        nc.sync.dma_start(out=gate_rest[:], in_=gate[:, GROUP:S])
+        gates = [gate_first[:]] + [gate_rest[:, g * GROUP : (g + 1) * GROUP] for g in range(3)]
         x_bytes = {}
-        for c in range(S // CHUNK):
+        for c in range(CHUNKS):
             u = int(c * CHUNK >= EARLY)
             x_bytes[c] = placed[u][:, c * CHUNK - spans[u][0] : (c + 1) * CHUNK - spans[u][0]]
 
-        raw = {("w1", 0): w1_first[:], ("w1", 1): w1_second[:], ("w3", 0): w3_first[:], ("w3", 1): w3_room[:, 0]}
         grouped, codes, scales = {}, {}, {}
         for name in ("w1", "w3"):
-            grouped[name] = lay([P, PACK, P, PACK], BF16, f"{name}_grouped", GROUPED_AT[name])
-            codes[name] = keep.tile([P, H], U32, name=f"{name}_codes", align_bytes=256)
-            scales[name] = keep.tile([P, H], U8, name=f"{name}_scales", align_bytes=256)
+            for t in (0, 2):
+                if name == "w3":
+                    grouped[name, t] = lay([P, 2, P, PACK], BF16, f"w3_grouped{t}", W3_GROUPED_AT[t])
+                else:
+                    grouped[name, t] = lay([P, 2, P, PACK], BF16, f"w1_grouped{t}", W1_GROUPED_AT + 1024 * t)
+            codes[name] = own([P, H], U32, f"{name}_codes")
+            scales[name] = own([P, H], U8, f"{name}_scales")
 
         def cast(name, u, t, on_vector):
-            src = raw[name, u].rearrange("p j (m t) -> p m j t", t=PACK)[:, :, :, t : t + 2]
-            to = grouped[name][:, :, 64 * u : 64 * (u + 1), :].rearrange("p t m j -> p m j t")[:, :, :, t : t + 2]
+            src = raw[name, u][:].rearrange("p j (m t) -> p m j t", t=PACK)[:, :, :, t : t + 2]
+            a, b = CUTS[name][u : u + 2]
+            to = grouped[name, t][:, :, a // PACK : b // PACK, :].rearrange("p t m j -> p m j t")
             if on_vector:
                 nc.vector.tensor_copy(to, src)
             else:
@@ -128,14 +143,16 @@ def tile_picked_route2_glusilu_p_kernel(
                 nc.vector.quantize_mx(
                     out=codes[name][:, t * P : (t + 2) * P].bitcast(FP8X4),
                     scales=scales[name][:, t * P : (t + 2) * P],
-                    in_=grouped[name][:, t : t + 2].rearrange("p t m j -> p (t m j)"),
+                    in_=grouped[name, t][:].rearrange("p t m j -> p (t m j)"),
                 )
 
         cast("w1", 0, 0, False)
         cast("w1", 0, 2, False)
-        cast("w1", 1, 0, True)
+        cast("w1", 1, 0, False)
         cast("w1", 1, 2, False)
         quantise("w1")
+        w2_raw = lay([P, PACK, N], F32, "w2_raw", W2_RAW_AT)
+        nc.scalar.dma_start(out=w2_raw[:], in_=w2.rearrange("(p j) c -> p j c", j=PACK))
         warm = psum.tile([P, 2 * GROUP], F32, name="warm", tag="bank7")
         for i, width in enumerate((GROUP, GROUP, GROUP, CHUNK)):
             nc.tensor.matmul_mx(
@@ -147,89 +164,96 @@ def tile_picked_route2_glusilu_p_kernel(
                 start=True,
                 stop=True,
             )
-        w2_raw = lay([P, PACK, N], F32, "w2_raw", GROUPED_AT["w1"])
-        nc.scalar.dma_start(out=w2_raw[:], in_=w2.rearrange("(p j) c -> p j c", j=PACK))
-        for first in (0, 2, 6):
-            words = keep.tile([P, 2 * CHUNK], U16, name=f"words{first}", align_bytes=256)
-            pick_words(range(first, first + 2), words)
-        gate_sb = lay([P, S], F32, "gate_sb", GATE_AT)
-        nc.sync.dma_start(out=gate_sb[:], in_=gate)
+        x_codes = {}
+
+        def pick_words(first, words):
+            pick(word_table, words, first * CHUNK, GROUP)
+            for i in (0, 1):
+                x_codes[first + i] = words[:, i * CHUNK : (i + 1) * CHUNK]
+
+        pick_words(0, lay([P, GROUP], U16, "words0", FIRST_WORDS_AT))
+        for first in (2, 4):
+            pick_words(first, own([P, GROUP], U16, f"words{first}"))
         cast("w3", 0, 0, False)
         cast("w3", 0, 2, False)
         cast("w3", 1, 0, True)
         cast("w3", 1, 2, True)
+        cast("w3", 2, 0, True)
+        cast("w3", 2, 2, True)
         quantise("w3")
-        pick_words(range(4, 6), lay([P, 2 * CHUNK], U16, "words_last", GROUPED_AT["w3"]))
+        pick_words(6, lay([P, GROUP], U16, "words6", LAST_WORDS_AT))
 
-        w2_codes = keep.tile([P, N], U32, name="w2_codes", align_bytes=256)
-        w2_scales = keep.tile([P, N], U8, name="w2_scales", align_bytes=256)
-        w2_grouped = lay([P, N, PACK], BF16, "w2_grouped", W3_SECOND_AT)
+        w2_scales = own([P, N], U8, "w2_scales")
+        w2_grouped = lay([P, N, PACK], BF16, "w2_grouped", W3_SECOND_AT + 512)
 
-        def product(name, c):
-            tag = f"bank{(W1_BANK if name == 'w1' else W3_BANK)[c]}"
-            bank = psum.tile([P, PACK, CHUNK], F32, name=f"{name}_bank{c}", tag=tag)
+        def product(name, c, bank_no, a=0, b=CHUNK):
+            bank = psum.tile([P, PACK, b - a], F32, name=f"{name}_bank{c}_{a}", tag=f"bank{bank_no}")
             for t in range(PACK):
                 nc.tensor.matmul_mx(
                     out=bank[:, t, :],
                     lhsT=codes[name][:, t * P : (t + 1) * P].bitcast(FP8X4),
                     lhsT_scale=scales[name][:, t * P : (t + 1) * P],
-                    rhs=x_codes[c].bitcast(FP4X4),
-                    rhs_scale=x_bytes[c],
+                    rhs=x_codes[c][:, a:b].bitcast(FP4X4),
+                    rhs_scale=x_bytes[c][:, a:b],
                     start=True,
                     stop=True,
                 )
             return bank[:].rearrange("p t n -> p n t")
 
-        h = {g: keep.tile([P, GROUP, PACK], BF16, name=f"h{g}", align_bytes=256) for g in (2, 3)}
-        h_first = [
-            lay([P, CHUNK, PACK], BF16, "h_first0", H_AT),
-            keep.tile([P, CHUNK, PACK], BF16, name="h_first1", align_bytes=256),
-        ]
-        y, acts, ups, weighted = {}, {}, {}, {}
+        y, acts, ups, weighted, h = {}, {}, {}, {}, {}
 
-        def activate(c):
-            a = product("w1", c)
-            if c in (2, 3):
-                acts[c] = lay([P, CHUNK, PACK], F32, f"act{c}", W3_SECOND_AT + (c - 1) * 4 * PACK * CHUNK)
+        def activate(c, b=CHUNK):
+            a = product("w1", c, W1_BANK[c], 0, b)
+            if c in ACT_AT:
+                acts[c] = lay([P, CHUNK, PACK], F32, f"act{c}", ACT_AT[c])
             else:
-                acts[c] = keep.tile([P, CHUNK, PACK], F32, name=f"act{c}", align_bytes=256)
-            if c == 6:
-                nc.scalar.activation(acts[c][:], a, SILU, bias=window[:, 0:1])
+                acts[c] = own([P, CHUNK, PACK], F32, f"act{c}")
+            if c == CHUNKS - 2:
+                nc.scalar.activation(acts[c][:, 0:b], a, SILU, bias=window[:, 0:1])
             else:
-                nc.scalar.activation(acts[c][:], a, SILU)
+                nc.scalar.activation(acts[c][:, 0:b], a, SILU)
 
         def up(c):
-            ups[c] = product("w3", c)
+            ups[c] = product("w3", c, W3_BANK[c])
 
         def hidden(c):
-            g, i = divmod(c, GROUP // CHUNK)
-            to = h_first[i][:] if g == 0 else h[g][:, i * CHUNK : (i + 1) * CHUNK, :]
-            nc.vector.tensor_tensor(to, ups[c], acts[c][:], MULT)
+            at = EVEN_AT if c % 2 == 0 else ODD_AT[c // 2]
+            h[c] = lay([P, CHUNK, PACK], BF16, f"h{c}", at)
+            nc.vector.tensor_tensor(h[c][:], ups[c], acts[c][:], MULT)
 
         def second(g):
-            h_codes = keep.tile([P, GROUP], U32, name=f"h_codes{g}", align_bytes=256)
-            h_scales = keep.tile([P, GROUP], U8, name=f"h_scales{g}", align_bytes=256)
-            y[g] = psum.tile([P, GROUP], F32, name=f"y{g}", tag="bank7")
-            pieces = [(h_first[0][:], 0, CHUNK), (h_first[1][:], CHUNK, GROUP)] if g == 0 else [(h[g][:], 0, GROUP)]
-            for values, a, b in pieces:
+            if g == 0:
+                even = own([P, CHUNK], U32, "h_codes0")
+            else:
+                even = lay([P, CHUNK], U32, f"h_codes{2 * g}", ODD_CODES_AT[g - 1] + 256)
+            if g < 3:
+                odd = lay([P, CHUNK], U32, f"h_codes{2 * g + 1}", ODD_CODES_AT[g])
+            else:
+                odd = own([P, CHUNK], U32, "h_codes7")
+            h_codes = [even, odd]
+            for i in (0, 1):
+                h_scales = own([P, CHUNK], U8, f"h_scales{2 * g + i}")
                 nc.vector.quantize_mx(
-                    out=h_codes[:, a:b].bitcast(FP8X4),
-                    scales=h_scales[:, a:b],
-                    in_=values.rearrange("p n t -> p (n t)"),
+                    out=h_codes[i][:].bitcast(FP8X4),
+                    scales=h_scales[:],
+                    in_=h[2 * g + i][:].rearrange("p n t -> p (n t)"),
                 )
+                y[2 * g + i] = psum.tile([P, CHUNK], F32, name=f"y{2 * g + i}", tag=f"bank{Y_BANK[2 * g + i]}")
                 nc.tensor.matmul_mx(
-                    out=y[g][:, a:b],
+                    out=y[2 * g + i][:],
                     lhsT=w2_codes[:].bitcast(FP8X4),
                     lhsT_scale=w2_scales[:],
-                    rhs=h_codes[:, a:b].bitcast(FP8X4),
-                    rhs_scale=h_scales[:, a:b],
+                    rhs=h_codes[i][:].bitcast(FP8X4),
+                    rhs_scale=h_scales[:],
                     start=True,
                     stop=True,
                 )
 
         def weigh(g):
-            weighted[g] = keep.tile([P, GROUP], F32, name=f"weighted{g}", align_bytes=256)
-            nc.vector.tensor_tensor(weighted[g][:], y[g][:], gate_sb[:, g * GROUP : (g + 1) * GROUP], MULT)
+            weighted[g] = own([P, GROUP], F32, f"weighted{g}")
+            for i in (0, 1):
+                cols = slice(i * CHUNK, (i + 1) * CHUNK)
+                nc.vector.tensor_tensor(weighted[g][:, cols], y[2 * g + i][:], gates[g][:, cols], MULT)
 
         def place(g):
             cols = slice(g * GROUP // PER_COL, (g + 1) * GROUP // PER_COL)
@@ -241,34 +265,39 @@ def tile_picked_route2_glusilu_p_kernel(
             w2_grouped[:].rearrange("p (c i) j -> p c j i", i=4),
             w2_raw[:].rearrange("p j (c i) -> p c j i", i=4),
         )
+        activate(2)
+        activate(3)
+        activate(4)
+        up(0)
+        up(1)
+        activate(5)
+        activate(6)
+        up(2)
+        activate(7, CHUNK // 2)
+        up(3)
+        hidden(0)
+        hidden(1)
+        w2_codes = lay([P, N], U32, "w2_codes", FIRST_WORDS_AT)
         nc.vector.quantize_mx(
             out=w2_codes[:].bitcast(FP8X4),
             scales=w2_scales[:],
             in_=w2_grouped[:].rearrange("p n j -> p (n j)"),
         )
-        activate(2)
-        activate(3)
-        up(0)
-        up(1)
-        activate(4)
-        activate(5)
-        hidden(0)
-        up(2)
-        activate(6)
-        hidden(1)
-        up(3)
         for g in range(4):
             second(g)
-            if g == 0:
-                activate(7)
-                h[1] = lay([P, GROUP, PACK], BF16, "h1", H_AT)
-            for c in range(2 * g + 2, min(2 * g + 4, 8)):
-                hidden(c)
-                if c + 2 < 8:
-                    up(c + 2)
+            if g < 3:
+                hidden(2 * g + 2)
+            if g < 2:
+                up(2 * g + 4)
             weigh(g)
-        for g in range(4):
             place(g)
+            if g == 0:
+                late = product("w1", 7, Y_BANK[1], CHUNK // 2, CHUNK)
+                nc.scalar.activation(acts[7][:, CHUNK // 2 : CHUNK], late, SILU)
+            if g < 3:
+                hidden(2 * g + 3)
+            if g < 2:
+                up(2 * g + 5)
 
         nc.sync.dma_start(out=out[:, 0 : U // 2], in_=window[:, 0 : U // 2])
         nc.scalar.dma_start(out=out[:, U // 2 : U], in_=window[:, U // 2 : U])

@@ -299,5 +299,4 @@ def tile_picked_route2_glusilu_p_kernel(
             if g < 2:
                 up(2 * g + 5)
 
-        nc.sync.dma_start(out=out[:, 0 : U // 2], in_=window[:, 0 : U // 2])
-        nc.scalar.dma_start(out=out[:, U // 2 : U], in_=window[:, U // 2 : U])
+        nc.scalar.dma_start(out=out, in_=window[:])

@@ -29,14 +29,14 @@ TOP = P - SCALE_ROWS
 EARLY = 6 * CHUNK
 EVEN_AT = 0
 W1_GROUPED_AT = 18432
-W2_RAW_AT = W1_GROUPED_AT
+W2_RAW_AT = W1_GROUPED_AT + 1024
 ODD_AT = (1024, 2048, 4096, 6144)
 ODD_CODES_AT = (2816, 4864, 6912)
-W3_SECOND_AT = 28672
-ACT_AT = {2: W3_SECOND_AT - 1536, 3: W3_SECOND_AT + 1536, 4: 8704}
-W3_GROUPED_AT = {0: 10240, 2: 13312}
+ACT_AT = {2: 8704, 3: 12544, 4: 15616}
+W2_GROUPED_AT = 14592
+W3_GROUPED_AT = {0: 10240, 2: 14336}
 LAST_WORDS_AT = 11264
-FIRST_WORDS_AT = 17408
+FIRST_WORDS_AT = 17920
 W1_BANK = (0, 1, 2, 3, 4, 2, 3, 4)
 W3_BANK = (6, 7, 0, 1, 0, 1, 0, 1)
 Y_BANK = (6, 7, 5, 2, 6, 3, 5, 2)
@@ -61,10 +61,7 @@ def tile_picked_route2_glusilu_p_kernel(
 
         def load_piece(name, w, u):
             a, b = CUTS[name][u : u + 2]
-            if (name, b) == ("w3", H):
-                raw[name, u] = lay([P, PACK, b - a], F32, "w3_last", W3_SECOND_AT)
-            else:
-                raw[name, u] = own([P, PACK, b - a], F32, f"{name}_raw{u}")
+            raw[name, u] = own([P, PACK, b - a], F32, f"{name}_raw{u}")
             nc.sync.dma_start(out=raw[name, u][:], in_=w[:, a:b].rearrange("(p j) c -> p j c", j=PACK))
 
         offs_sb = keep.tile([P, S // PER_COL], U16, name="offs_sb")
@@ -184,7 +181,7 @@ def tile_picked_route2_glusilu_p_kernel(
         pick_words(6, lay([P, GROUP], U16, "words6", LAST_WORDS_AT))
 
         w2_scales = own([P, N], U8, "w2_scales")
-        w2_grouped = lay([P, N, PACK], BF16, "w2_grouped", W3_SECOND_AT + 512)
+        w2_grouped = lay([P, N, PACK], BF16, "w2_grouped", W2_GROUPED_AT)
 
         def product(name, c, bank_no, a=0, b=CHUNK):
             bank = psum.tile([P, PACK, b - a], F32, name=f"{name}_bank{c}_{a}", tag=f"bank{bank_no}")
@@ -261,12 +258,12 @@ def tile_picked_route2_glusilu_p_kernel(
 
         activate(0)
         activate(1)
+        activate(2)
+        activate(3)
         nc.scalar.copy(
             w2_grouped[:].rearrange("p (c i) j -> p c j i", i=4),
             w2_raw[:].rearrange("p j (c i) -> p c j i", i=4),
         )
-        activate(2)
-        activate(3)
         activate(4)
         up(0)
         up(1)

from contextlib import ExitStack

import concourse.mybir as mybir

K, T, S, H, N, U = 512, 2048, 1024, 512, 128, 2048
FLOPS = 2 * S * (2 * K * H + H * N)

F32 = mybir.dt.float32
BF16 = mybir.dt.bfloat16
I32 = mybir.dt.int32
U32 = mybir.dt.uint32
U16 = mybir.dt.uint16
U8 = mybir.dt.uint8
FP8X4 = mybir.dt.float8_e4m3fn_x4
FP4X4 = mybir.dt.float4_e2m1fn_x4
SILU = mybir.ActivationFunctionType.Silu
COPY = mybir.ActivationFunctionType.Copy
MULT = mybir.AluOpType.mult

P = 128
PACK = 4
PER_COL = 16
CHUNK = 128
CHUNKS = S // CHUNK
GROUP = 256
CUTS = {"w1": (0, 256, 512), "w3": (0, 192, 384, 512)}
SCALE_ROWS = 16
TOP = P - SCALE_ROWS
EARLY = 6 * CHUNK
EVEN_AT = 0
W1_GROUPED_AT = 18432
W2_RAW_AT = W1_GROUPED_AT + 1024
ODD_AT = (1024, 2048, 4096, 6144)
ODD_CODES_AT = (2816, 4864, 6912)
ACT_AT = {2: 8704, 3: 12544, 4: 15616}
W2_GROUPED_AT = 14592
W3_GROUPED_AT = {0: 10240, 2: 14336}
LAST_WORDS_AT = 11264
FIRST_WORDS_AT = 17920
W1_BANK = (0, 1, 2, 3, 4, 2, 3, 4)
W3_BANK = (6, 7, 0, 1, 0, 1, 0, 1)
Y_BANK = (6, 7, 5, 2, 6, 3, 5, 2)


def tile_picked_route2_glusilu_p_kernel(
    tc, x_words, x_scales, gate, w1, w3, w2, offs, dst, out
):
    nc = tc.nc
    with ExitStack() as ctx:
        keep = ctx.enter_context(tc.tile_pool(name="keep", bufs=1))
        laid = ctx.enter_context(tc.tile_pool(name="laid", bufs=1))
        psum = ctx.enter_context(tc.psum_pool(name="psum", bufs=1))

        def lay(shape, dtype, name, offset):
            return laid.tile(shape, dtype, name=name, offset=offset, align_bytes=256)

        def own(shape, dtype, name):
            return keep.tile(shape, dtype, name=name, align_bytes=256)

        raw = {}

        def load_piece(name, w, u):
            a, b = CUTS[name][u : u + 2]
            raw[name, u] = own([P, PACK, b - a], F32, f"{name}_raw{u}")
            nc.sync.dma_start(out=raw[name, u][:], in_=w[:, a:b].rearrange("(p j) c -> p j c", j=PACK))

        offs_sb = keep.tile([P, S // PER_COL], U16, name="offs_sb")
        dst_sb = keep.tile([P, S // PER_COL], U16, name="dst_sb")
        word_table = own([P, T], U16, "word_table")
        scale_table = own([P, T], U8, "scale_table")
        window = own([P, U], F32, "window")
        zeros = keep.tile([P, 8], F32, name="zeros")
        spans = ((0, EARLY), (EARLY, S - EARLY))
        picked = [own([P, n], U8, f"picked{at}") for at, n in spans]
        placed = [own([P, n], U8, f"placed{at}") for at, n in spans]

        nc.sync.dma_start(offs_sb[:], offs)
        nc.sync.dma_start(out=scale_table[TOP:P, :].bitcast(I32), in_=x_scales[0].bitcast(I32))
        load_piece("w1", w1, 0)
        load_piece("w1", w1, 1)
        nc.sync.dma_start(out=word_table[:].bitcast(I32), in_=x_words[0].bitcast(I32))
        load_piece("w3", w3, 0)

        nc.vector.memset(zeros[:], 0.0)
        nc.vector.memset(scale_table[0:TOP, :].bitcast(I32), 0)
        for tile in placed:
            nc.vector.memset(tile[:].bitcast(I32), 0)
        nc.scalar.activation(window[:, 0 : U // 2], zeros[:, 0:1].to_broadcast([P, U // 2]), SILU)
        nc.vector.memset(window[:, U // 2 : U], 0.0)

        def pick(table, tile, first, count):
            cols = slice(first // PER_COL, (first + count) // PER_COL)
            nc.vector.tensor_copy(tile[:], table[:].indirect(offs_sb[:, cols]))

        def move_rows(u):
            for q in (0, 2, 1, 3):
                nc.sync.dma_start(
                    out=placed[u][32 * q : 32 * q + 4, :].bitcast(I32),
                    in_=picked[u][TOP + 4 * q : TOP + 4 * q + 4, :].bitcast(I32),
                )

        pick(scale_table, picked[0], *spans[0])
        move_rows(0)
        load_piece("w3", w3, 1)
        load_piece("w3", w3, 2)
        pick(scale_table, picked[1], *spans[1])
        move_rows(1)
        gate_first = own([P, GROUP], F32, "gate_first")
        nc.sync.dma_start(out=gate_first[:], in_=gate[:, 0:GROUP])
        gate_rest = own([P, S - GROUP], F32, "gate_rest")
        nc.sync.dma_start(dst_sb[:], dst)
        nc.sync.dma_start(out=gate_rest[:], in_=gate[:, GROUP:S])
        gates = [gate_first[:]] + [gate_rest[:, g * GROUP : (g + 1) * GROUP] for g in range(3)]
        x_bytes = {}
        for c in range(CHUNKS):
            u = int(c * CHUNK >= EARLY)
            x_bytes[c] = placed[u][:, c * CHUNK - spans[u][0] : (c + 1) * CHUNK - spans[u][0]]

        grouped, codes, scales = {}, {}, {}
        for name in ("w1", "w3"):
            for t in (0, 2):
                if name == "w3":
                    grouped[name, t] = lay([P, 2, P, PACK], BF16, f"w3_grouped{t}", W3_GROUPED_AT[t])
                else:
                    grouped[name, t] = lay([P, 2, P, PACK], BF16, f"w1_grouped{t}", W1_GROUPED_AT + 1024 * t)
            codes[name] = own([P, H], U32, f"{name}_codes")
            scales[name] = own([P, H], U8, f"{name}_scales")

        def cast(name, u, t, on_vector):
            src = raw[name, u][:].rearrange("p j (m t) -> p m j t", t=PACK)[:, :, :, t : t + 2]
            a, b = CUTS[name][u : u + 2]
            to = grouped[name, t][:, :, a // PACK : b // PACK, :].rearrange("p t m j -> p m j t")
            if on_vector:
                nc.vector.tensor_copy(to, src)
            else:
                nc.scalar.copy(to, src)

        def quantise(name):
            for t in (0, 2):
                nc.vector.quantize_mx(
                    out=codes[name][:, t * P : (t + 2) * P].bitcast(FP8X4),
                    scales=scales[name][:, t * P : (t + 2) * P],
                    in_=grouped[name, t][:].rearrange("p t m j -> p (t m j)"),
                )

        cast("w1", 0, 0, False)
        cast("w1", 0, 2, False)
        cast("w1", 1, 0, False)
        cast("w1", 1, 2, False)
        quantise("w1")
        w2_raw = lay([P, PACK, N], F32, "w2_raw", W2_RAW_AT)
        nc.scalar.dma_start(out=w2_raw[:], in_=w2.rearrange("(p j) c -> p j c", j=PACK))
        warm = psum.tile([P, 2 * GROUP], F32, name="warm", tag="bank7")
        for i, width in enumerate((GROUP, GROUP, GROUP, CHUNK)):
            nc.tensor.matmul_mx(
                out=warm[:, i % 2 * GROUP : i % 2 * GROUP + width],
                lhsT=codes["w1"][:, 0:P].bitcast(FP8X4),
                lhsT_scale=scales["w1"][:, 0:P],
                rhs=codes["w1"][:, 0:width].bitcast(FP8X4),
                rhs_scale=scales["w1"][:, 0:width],
                start=True,
                stop=True,
            )
        x_codes = {}

        def pick_words(first, words):
            pick(word_table, words, first * CHUNK, GROUP)
            for i in (0, 1):
                x_codes[first + i] = words[:, i * CHUNK : (i + 1) * CHUNK]

        pick_words(0, lay([P, GROUP], U16, "words0", FIRST_WORDS_AT))
        for first in (2, 4):
            pick_words(first, own([P, GROUP], U16, f"words{first}"))
        cast("w3", 0, 0, False)
        cast("w3", 0, 2, False)
        cast("w3", 1, 0, True)
        cast("w3", 1, 2, True)
        cast("w3", 2, 0, True)
        cast("w3", 2, 2, True)
        quantise("w3")
        pick_words(6, lay([P, GROUP], U16, "words6", LAST_WORDS_AT))

        w2_scales = own([P, N], U8, "w2_scales")
        w2_grouped = lay([P, N, PACK], BF16, "w2_grouped", W2_GROUPED_AT)

        def product(name, c, bank_no, a=0, b=CHUNK):
            bank = psum.tile([P, PACK, b - a], F32, name=f"{name}_bank{c}_{a}", tag=f"bank{bank_no}")
            for t in range(PACK):
                nc.tensor.matmul_mx(
                    out=bank[:, t, :],
                    lhsT=codes[name][:, t * P : (t + 1) * P].bitcast(FP8X4),
                    lhsT_scale=scales[name][:, t * P : (t + 1) * P],
                    rhs=x_codes[c][:, a:b].bitcast(FP4X4),
                    rhs_scale=x_bytes[c][:, a:b],
                    start=True,
                    stop=True,
                )
            return bank[:].rearrange("p t n -> p n t")

        y, acts, ups, weighted, h = {}, {}, {}, {}, {}

        def activate(c, b=CHUNK):
            a = product("w1", c, W1_BANK[c], 0, b)
            if c in ACT_AT:
                acts[c] = lay([P, CHUNK, PACK], F32, f"act{c}", ACT_AT[c])
            else:
                acts[c] = own([P, CHUNK, PACK], F32, f"act{c}")
            if c == CHUNKS - 2:
                nc.scalar.activation(acts[c][:, 0:b], a, SILU, bias=window[:, 0:1])
            else:
                nc.scalar.activation(acts[c][:, 0:b], a, SILU)

        def up(c):
            ups[c] = product("w3", c, W3_BANK[c])

        def hidden(c):
            at = EVEN_AT if c % 2 == 0 else ODD_AT[c // 2]
            h[c] = lay([P, CHUNK, PACK], BF16, f"h{c}", at)
            nc.vector.tensor_tensor(h[c][:], ups[c], acts[c][:], MULT)

        def second(g):
            if g == 0:
                even = own([P, CHUNK], U32, "h_codes0")
            else:
                even = lay([P, CHUNK], U32, f"h_codes{2 * g}", ODD_CODES_AT[g - 1] + 256)
            if g < 3:
                odd = lay([P, CHUNK], U32, f"h_codes{2 * g + 1}", ODD_CODES_AT[g])
            else:
                odd = own([P, CHUNK], U32, "h_codes7")
            h_codes = [even, odd]
            for i in (0, 1):
                h_scales = own([P, CHUNK], U8, f"h_scales{2 * g + i}")
                nc.vector.quantize_mx(
                    out=h_codes[i][:].bitcast(FP8X4),
                    scales=h_scales[:],
                    in_=h[2 * g + i][:].rearrange("p n t -> p (n t)"),
                )
                y[2 * g + i] = psum.tile([P, CHUNK], F32, name=f"y{2 * g + i}", tag=f"bank{Y_BANK[2 * g + i]}")
                nc.tensor.matmul_mx(
                    out=y[2 * g + i][:],
                    lhsT=w2_codes[:].bitcast(FP8X4),
                    lhsT_scale=w2_scales[:],
                    rhs=h_codes[i][:].bitcast(FP8X4),
                    rhs_scale=h_scales[:],
                    start=True,
                    stop=True,
                )

        def weigh(g):
            weighted[g] = own([P, GROUP], F32, f"weighted{g}")
            for i in (0, 1):
                cols = slice(i * CHUNK, (i + 1) * CHUNK)
                nc.vector.tensor_tensor(weighted[g][:, cols], y[2 * g + i][:], gates[g][:, cols], MULT)

        def place(g):
            cols = slice(g * GROUP // PER_COL, (g + 1) * GROUP // PER_COL)
            nc.scalar.activation(window[:].indirect(dst_sb[:, cols]), weighted[g][:], COPY)

        activate(0)
        activate(1)
        activate(2)
        activate(3)
        nc.scalar.copy(
            w2_grouped[:].rearrange("p (c i) j -> p c j i", i=4),
            w2_raw[:].rearrange("p j (c i) -> p c j i", i=4),
        )
        activate(4)
        up(0)
        up(1)
        activate(5)
        activate(6)
        up(2)
        activate(7, CHUNK // 2)
        up(3)
        hidden(0)
        hidden(1)
        w2_codes = lay([P, N], U32, "w2_codes", FIRST_WORDS_AT)
        nc.vector.quantize_mx(
            out=w2_codes[:].bitcast(FP8X4),
            scales=w2_scales[:],
            in_=w2_grouped[:].rearrange("p n j -> p (n j)"),
        )
        for g in range(4):
            second(g)
            if g < 3:
                hidden(2 * g + 2)
            if g < 2:
                up(2 * g + 4)
            weigh(g)
            place(g)
            if g == 0:
                late = product("w1", 7, Y_BANK[1], CHUNK // 2, CHUNK)
                nc.scalar.activation(acts[7][:, CHUNK // 2 : CHUNK], late, SILU)
            if g < 3:
                hidden(2 * g + 3)
            if g < 2:
                up(2 * g + 5)

        nc.scalar.dma_start(out=out, in_=window[:])
